import numpy as np, ml_dtypes
CORES = [16,17,18,19,32,33,34,35]
N = 8
BF = ml_dtypes.bfloat16
def gentries(a):
    return np.ascontiguousarray(a.reshape(8, 16, -1).transpose(0, 2, 1)).reshape(8, -1)
def gtable(e):
    e = np.asarray(e); return np.ascontiguousarray(e.reshape(8, -1, 16).transpose(0, 2, 1)).reshape(128, -1).astype(np.int32)
def f(rng, *shape):
    return (rng.standard_normal(shape, dtype=np.float32) * np.exp2(rng.integers(-2, 3, shape[:-1] + (1,)))).astype(BF)
def wide(rng, *shape):
    v = f(rng, *shape).astype(np.float32); k = shape[:-2] + (1, shape[-1])
    return (v * np.exp2(rng.integers(-6, 7, k)) * (rng.random(k) > 0.0625)).astype(BF)
V, D, C, R = 2048, 4, 48, 2
def ranks(t):
    return t.reshape(8, D, N, V).transpose(2, 0, 1, 3)
def globe(a, bl):
    out = np.zeros((N, 8, D * V), np.int64)
    for r in range(N):
        own = np.broadcast_to(r * V + np.arange(V), (8, V))
        ghosts = (np.arange(N)[:, None, None] * V + bl[:, :, r]).transpose(1, 0, 2).reshape(8, N * C)
        out[r] = np.take_along_axis(np.concatenate([own, ghosts], 1), a[r].reshape(8, D * V).astype(np.int64), 1)
    return out.reshape(N, 8, D, V).transpose(1, 2, 0, 3).reshape(8, D, N * V)
def unpack(nb, bl):
    return np.stack([gentries(t) for t in nb]).reshape(N, 8, D, V), np.stack([gentries(t) for t in bl]).reshape(N, 8, N, C)
def pack(rng, a, bl, v):
    o = np.argsort(rng.random(a.shape), 2); a = np.take_along_axis(a, o, 2); v = np.take_along_axis(v, o, 2)
    return {"nb": np.stack([gtable(t.reshape(8, D * V)) for t in a]), "bl": np.stack([gtable(t.reshape(8, N * C)) for t in bl]),
            "w": np.ascontiguousarray(v).reshape(N, 8, D * V).astype(np.float32).astype(BF), "x": f(rng, N, 128, V)}
def graphs(rng, p):
    bl = np.argsort(rng.random((N, 8, N, V)), axis=-1)[..., :C]
    a = np.full((N, 8, D, V), -1, np.int64)
    for g in range(8):
        for d in range(D):
            for r in range(N):
                for q in range(r):
                    o = rng.permutation(C); u = bl[r, g, q]; t = bl[q, g, r][o]
                    k = (a[r, g, d, u] < 0) & (a[q, g, d, t] < 0) & (rng.random(C) < p)
                    a[r, g, d, u[k]] = V + q * C + o[k]; a[q, g, d, t[k]] = V + r * C + np.flatnonzero(k)
            for r in range(N):
                e = rng.permutation(np.flatnonzero(a[r, g, d] < 0)); h = len(e) // 2
                a[r, g, d, e[:h]] = e[h:2 * h]; a[r, g, d, e[h:2 * h]] = e[:h]
                if len(e) > 2 * h: a[r, g, d, e[-1]] = (e[-1] + 1) % V
        for r in range(N):
            alias = np.full(V, -1, np.int64); alias[bl[r, g, r]] = V + r * C + np.arange(C)
            b = a[r, g]; n = np.where(b < V, alias[np.minimum(b, V - 1)], -1)
            a[r, g] = np.where((n >= 0) & (rng.random((D, V)) < 0.5), n, b)
    return a, bl
def both(a, bl, z):
    return np.array(ranks(np.take_along_axis(z, np.minimum(globe(a, bl), np.arange(N * V)), 2)))
def setup_inputs(rng):
    a, bl = graphs(rng, 0.6)
    return pack(rng, a, bl, both(a, bl, np.exp2(4 * rng.random((8, D, N * V)))))
def setup_inputs_ties(rng):
    a, bl = graphs(rng, 0.6); z = rng.integers(1, 4, (8, D, N * V)).astype(np.float64); z[rng.integers(0, 8)] = 1
    z *= np.exp2(rng.integers(-20, 21, (8, 1, 1)))
    return pack(rng, a, bl, both(a, bl, z))
def setup_inputs_borders(rng):
    a, bl = graphs(rng, 1.0); v = both(a, bl, np.exp2(3 * rng.random((8, D, N * V))))
    far = ranks(globe(a, bl) // V != np.arange(N * V) // V)
    return pack(rng, a, bl, v * np.where(far, 8, 1))
def setup_inputs_hubs(rng):
    a, bl = graphs(rng, 0.6); v = both(a, bl, np.exp2(4 * rng.random((8, D, N * V))))
    for r in range(N):
        for g in range(8):
            e = rng.permutation(V); h = e[:16]; leaves = e[16:V // 2]; b = a[r, g]; c = v[r, g]
            b[:, leaves] = h[rng.integers(0, 16, (D, len(leaves)))]
            b[0, h] = h[np.arange(16) ^ 1]; c[0, h] = 256
    return pack(rng, a, bl, v)
def setup_inputs_any(rng):
    bl = rng.integers(0, V, (N, 8, N, C)); bl[..., C // 2:] = bl[..., :1]; bl[..., 1] = 0; bl[..., 2] = V - 1
    a = rng.integers(0, V + N * C, (N, 8, D, V)); j = np.arange(V)
    a = np.where(ranks(globe(a, bl) == np.arange(N * V)), (j + 1) % V, a)
    o = rng.permutation(8); a[:, o[0]] = (j + 1) % V; a[:, o[1]] = j ^ 1
    for r in range(N):
        for g in o[2:5]:
            q = r ^ 1
            a[r, g, :, bl[r, g, q, 0]] = V + q * C + rng.choice(np.r_[0, C // 2:C], D)
    return pack(rng, a, bl, np.exp2(4 * rng.random((N, 8, D, V))))
def setup_inputs_spread(rng):
    a, bl = graphs(rng, 0.6); z = np.exp2(rng.integers(-3, 4, (8, D, N * V)) + rng.random((8, D, N * V)))
    d = pack(rng, a, bl, both(a, bl, z)); d["x"] = wide(rng, N, 128, V); return d
def check_inputs(d):
    bad = []
    if d["bl"].min() < 0 or d["bl"].max() >= V: bad.append("bl")
    if d["nb"].min() < 0 or d["nb"].max() >= V + N * C: bad.append("nb")
    if not bad and (globe(*unpack(d["nb"], d["bl"])) == np.arange(N * V)).any(): bad.append("own neighbour")
    u = d["w"].astype(np.float32)
    if not (np.isfinite(u).all() and (u > 0).all()): bad.append("w")
    v = np.abs(d["x"].astype(np.float32))
    if not np.isfinite(v).all(): bad.append("x")
    if not 4.0 * D * float(u.max()) * float(v.max()) < 2.0 ** 127: bad.append("range")
    return bad
def reference(nb, bl, w, x):
    i = np.arange(N * V); A = globe(*unpack(nb, bl))
    u = w.astype(np.float64).reshape(N, 8, D, V).transpose(1, 2, 0, 3).reshape(8, D, N * V)
    mate = np.tile(i, (8, 1)); free = np.ones((8, N * V), bool)
    for t in range(R):
        k = np.where(np.take_along_axis(free[:, None], A, 2), u, 0.0)
        P = np.take_along_axis(A, np.argmax(k, 1)[:, None], 1)[:, 0]
        P = np.where(free & (np.max(k, 1) > 0), P, -1)
        hit = (P >= 0) & (np.take_along_axis(P, np.maximum(P, 0), 1) == i)
        mate = np.where(hit, P, mate); free = free & ~hit
    two = mate != i; first = np.minimum(mate, i); rep = first == i
    num = (np.add.accumulate(rep.reshape(8, N, V).astype(np.int64), 2) - 1 + V * np.arange(N)[:, None]).reshape(8, N * V)
    cm = np.take_along_axis(num, first, 1).reshape(8, N, V)
    xx = np.ascontiguousarray(x.astype(np.float64).reshape(N, 8, 16, V).transpose(1, 2, 0, 3)).reshape(8, 16, N * V)
    X = xx + np.where(two[:, None], np.take_along_axis(xx, mate[:, None], 2), 0.0)
    s = np.zeros((8, 16, N * V))
    for d in range(D):
        s += u[:, d, None] * np.take_along_axis(X, A[:, d, None], 2)
    s = s + np.where(two[:, None], np.take_along_axis(s, mate[:, None], 2), 0.0)
    y = np.zeros((8, 16, N * V))
    for g in range(8):
        y[g][:, num[g, rep[g]]] = s[g][:, rep[g]]
    y = np.ascontiguousarray(y.reshape(8, 16, N, V).transpose(2, 0, 1, 3)).reshape(N, 128, V)
    return {"y": y.astype(np.float32), "cm": np.stack([gtable(cm[:, r]) for r in range(N)]).astype(np.float32)}

@@ -1,0 +1,538 @@
+from concourse.bass import DstId, RemoteDMATransfer
+from concourse.mybir import AluOpType as Op, ActivationFunctionType as Fn
+
+N, V, D, C = 8, 2048, 4, 48
+NG = N * C
+SH = 16
+G0 = SH + V
+TB = G0 + NG
+BIG = 4096
+BK = 32768
+
+_F, _B, _I, _H, _U = "float32", "bfloat16", "int32", "float16", "uint16"
+_LOG = {n: (w, t) for n, w, t in [
+    ("pf", 1, _F), ("pi", 1, _I), ("ci", 1, _I), ("cf", 1, _F), ("c1000", 1, _F), ("p16", 1, _F), ("pX", 1, _F), ("pE", 1, _F),
+    ("jj", 144, _F), ("jm", 128, _F), ("v16", 128, _F), ("vB", 128, _F), ("basec", 24, _F), ("cols", 16, _F), ("mc", 16, _F),
+    ("idb", 128, _B), ("idf", 128, _F), ("e16", 128, _B), ("ip", 128, _B), ("inn", 128, _B), ("gsh", 144, _H), ("gsf", 144, _F),
+    ("hb", 144, _B), ("hh", 144, _H), ("hf", 144, _F), ("gb", 128, _B), ("tri0", 128, _B), ("tri", 128, _B), ("rm", 2048, _H),
+    ("zz", 128, _F), ("gid", TB, _F), ("od", 400, _F),
+    ("wr", 8192, _B), ("nbi", 512, _I), ("bli", 24, _I), ("xw", TB, _B), ("xo", V, _B), ("wa", 8192, _B),
+    ("nbu", 512, _U), ("nbc", 512, _F), ("blu", 24, _U), ("blh", 24, _I), ("blx", 24, _U), ("bll", 24, _I), ("blo", 24, _U),
+    ("gidb", NG, _F), ("mask", NG, _F), ("xb", NG, _B),
+    ("wT", 384, _F), ("gt", 768, _B), ("code", 512, _F), ("h1", 256, _F), ("q1", 128, _I), ("l1i", 128, _I), ("l1u", 128, _U),
+    ("l1s", 128, _F), ("l1f", 128, _F), ("lm", NG, _H), ("l1b", 24, _F), ("l1bu", 24, _U), ("land1", 24, _F), ("d1", 24, _F),
+    ("lu1", 24, _U), ("se1", 4, _U), ("ptab1", TB, _F), ("f1b", NG, _B), ("m1b", NG, _B), ("z1b", NG, _B), ("ftab", TB, _B),
+    ("m1B", 128, _F), ("l1m", 128, _F), ("cmk", 1536, _F), ("codeb", 96, _F), ("nbbi", 96, _I), ("nbba", 96, _I), ("nbbu", 96, _U),
+    ("wb", 1536, _B),
+    ("fb", 1536, _B), ("kb", 96, _F), ("h2b", 48, _F), ("q2b", 24, _I), ("l2bi", 24, _I), ("l2b", 24, _F), ("l2bu", 24, _U),
+    ("fl", 8192, _B), ("key", 512, _F), ("h2", 256, _F), ("q2", 128, _I), ("l2i", 128, _I), ("l2u", 128, _U), ("l2f", 128, _F),
+    ("land2", 24, _F), ("d2", 24, _F), ("lu2", 24, _U), ("se2", 4, _U), ("ptab2", TB, _F),
+    ("m2b", NG, _B), ("y2b", NG, _B), ("t2b", NG, _B), ("xmb", NG, _B), ("xm", NG, _B),
+    ("pp2", 2048, _H), ("m2B", 128, _F), ("m2l", 128, _F), ("mu", 128, _U),
+    ("mg", 2048, _H), ("rep", 128, _B), ("sc", 128, _F), ("nin", 128, _F), ("na", 128, _F), ("nm", 128, _F), ("numh", 128, _H),
+    ("numf", 128, _F), ("po", 128, _F), ("posu", 128, _U), ("numt", TB, _F), ("numb", NG, _F), ("cmo", 128, _F),
+    ("xt", TB, _F), ("qb", NG, _F), ("sb", NG, _F), ("st", TB, _F),
+    ("g2", 2048, _F), ("g3", 2048, _F), ("uu", 2048, _F), ("yw", 4096, _F),
+]}
+_WHERE, SCRATCH, _fill = {}, {}, {}
+for _n, (_w, _t) in _LOG.items():
+    if _w <= 512:
+        _WHERE[_n] = ("pack_" + _t, _fill.get(_t, 0))
+        _fill[_t] = _fill.get(_t, 0) + (_w + 15) // 16 * 16
+    else:
+        _WHERE[_n] = (_n, 0)
+        SCRATCH[_n] = ("sbuf", [128, _w], _t)
+for _t, _w in _fill.items():
+    SCRATCH["pack_" + _t] = ("sbuf", [128, _w], _t)
+_PSUM = {"k%d" % _i: 512 for _i in range(8)}
+for _n, _w in _PSUM.items():
+    SCRATCH[_n] = ("psum", [128, _w], _F)
+    _WHERE[_n] = (_n, 0)
+    _LOG[_n] = (_w, _F)
+NPOOL = 120
+SEMAPHORES = ["e%d" % k for k in range(7)] + ["sent"] + ["s%d" % i for i in range(NPOOL)]
+
+
+def a(name, c0=0, c1=None, cs=1, p0=0, p1=128, ps=1):
+    return (name, c0, _LOG[name][0] if c1 is None else c1, cs, p0, p1, ps)
+
+
+def ind(win, off):
+    return ("ind", win, off)
+
+
+def _clash(s, t):
+    if s[0] != t[0]:
+        return False
+    if not (s[1] < t[2] and t[1] < s[2] and s[4] < t[5] and t[4] < s[5]):
+        return False
+    if s[3] == t[3] > 1 and (s[1] - t[1]) % s[3]:
+        return False
+    if s[6] == t[6] > 1 and (s[4] - t[4]) % s[6]:
+        return False
+    return True
+
+
+def _plan(src, topo, cores):
+    used, out = set(), {}
+    for far in (True, False):
+        for dst in cores:
+            if dst == src or (topo.chip(dst) != topo.chip(src)) != far:
+                continue
+            free = [x for x in topo.engines(src, dst) if x not in used]
+            e = free[:2] if far else free[-2:]
+            used.update(e)
+            out[dst] = e
+    return out
+
+
+def rank_program(g, core, T, topo):
+    r = T.rank_of(core)
+    if r is None:
+        return
+    ops, acc = [], {}
+    mmgroup = {}
+    eng = {"v": g.vector, "s": g.scalar, "t": g.tensor, "g": g, "y": g.sync}
+
+    def ap(s):
+        if isinstance(s, tuple):
+            if s[0] == "ind":
+                return ap(s[1]).indirect(ap(s[2]))
+            name, b = _WHERE[s[0]]
+            cols = slice(b + s[1], b + s[2], s[3]) if s[3] > 1 else slice(b + s[1], b + s[2])
+            return T[name][slice(s[4], s[5], s[6]) if s[6] > 1 else slice(s[4], s[5]), cols]
+        return s
+
+    def regs(xs):
+        out = []
+        for s in xs:
+            if isinstance(s, tuple):
+                out += [s[1], s[2]] if s[0] == "ind" else [s]
+        return out
+
+    def op(q, fn, outs, ins, inc=1, stop=None):
+        i = len(ops)
+        wr, rd = [], regs(ins)
+        for o in outs:
+            if o[0] == "ind":
+                wr.append(o[1])
+                rd.append(o[2])
+            else:
+                wr.append(o)
+        dep = set()
+        for lst, w in ((rd, False), (wr, True)):
+            for s in lst:
+                for j, jw, t in acc.get(s[0], ()):
+                    if q == "t" and ops[j]["q"] == "t":
+                        continue
+                    if (s[0] in _PSUM and ops[j]["q"] != q) or ((w or jw) and _clash(s, t)):
+                        dep.add(j)
+        for lst, w in ((rd, False), (wr, True)):
+            for s in lst:
+                acc.setdefault(s[0], []).append((i, w, s))
+        ops.append({"q": q, "fn": fn, "dep": dep, "inc": inc, "sem": None, "waits": [], "K": 0})
+        if q == "t":
+            mmgroup.setdefault("open", []).append(i)
+            if stop:
+                for j in mmgroup["open"]:
+                    mmgroup[j] = i
+                mmgroup["open"] = []
+        return i
+
+    def tt(out, x, y, o):
+        op("v", lambda: g.vector.tensor_tensor(out=ap(out), in0=ap(x), in1=ap(y), op=o), [out], [x, y])
+
+    def ts(out, x, s1, o1, s2=None, o2=None):
+        if o2 is None:
+            op("v", lambda: g.vector.tensor_scalar(out=ap(out), in0=ap(x), scalar1=ap(s1), scalar2=None, op0=o1), [out], [x, s1])
+        else:
+            op("v", lambda: g.vector.tensor_scalar(out=ap(out), in0=ap(x), scalar1=ap(s1), scalar2=ap(s2), op0=o1, op1=o2),
+               [out], [x, s1, s2])
+
+    def tc(out, x):
+        op("v", lambda: g.vector.tensor_copy(out=ap(out), in_=ap(x)), [out], [x])
+
+    def ms(out, c):
+        op("v", lambda: g.vector.memset(ap(out), c), [out], [])
+
+    def act(out, x, scale=None, bias=None):
+        if scale is not None:
+            op("s", lambda: g.scalar.activation(out=ap(out), in_=ap(x), func=Fn.Copy, scale=ap(scale)), [out], [x, scale])
+        elif bias is not None:
+            op("s", lambda: g.scalar.activation(out=ap(out), in_=ap(x), func=Fn.Identity, bias=bias), [out], [x])
+        else:
+            op("s", lambda: g.scalar.activation(out=ap(out), in_=ap(x), func=Fn.Copy), [out], [x])
+
+    def mm(out, l, rr, start=True, stop=True):
+        op("t", lambda: g.tensor.matmul(ap(out), ap(l), ap(rr), start, stop), [out], [l, rr], stop=stop)
+
+    def iota(out, pattern, base, cm):
+        if _LOG[out[0]][1] != _I:
+            op("g", lambda: g.iota(ap(out), pattern, base, cm, allow_small_or_imprecise_dtypes=True), [out], [])
+        else:
+            op("g", lambda: g.iota(ap(out), pattern, base, cm), [out], [])
+
+    def dma(q, out, x):
+        f = lambda s: ap(s) if isinstance(s, tuple) else s()
+        return op(q, lambda: eng[q].dma_start(out=f(out), in_=f(x)), [out] if isinstance(out, tuple) else [], regs([x]), inc=16)
+
+    plan = _plan(core, topo, T.cores)
+    expect = sum(len(_plan(c, topo, T.cores)[core]) for c in T.cores if c != core)
+    sent = [0]
+
+    def slot(name, q, w, base=0):
+        return a(name, base + w * q, base + w * q + w)
+
+    def arrive(k, name, w, base=0):
+        i = len(ops)
+        for q in range(N):
+            if q != r:
+                acc.setdefault(name, []).append((i, True, slot(name, q, w, base)))
+        ops.append({"q": "r", "fn": None, "dep": set(), "inc": expect, "sem": "e%d" % k, "waits": [], "K": 0})
+
+    def send(k, name, w, dname, base=0):
+        dst = slot(dname, r, w, base)
+
+        def fn():
+            tr = []
+            for q in range(N):
+                if q != r:
+                    rid, pid, _se = topo.addr(T.cores[q])
+                    tr.append(RemoteDMATransfer(dst_ids=[DstId(rid=rid, pnc=pid)], dma_engine_mask=sum(1 << e for e in plan[T.cores[q]]),
+                                                remote_sem=T.sem["e%d" % k], src=ap(slot(name, q, w)), dst=ap(dst)))
+            g.remote_dma_fused(tr, local_sem=T.sem["sent"])
+            sent[0] += sum(len(e) for e in plan.values())
+        op("g", fn, [], [slot(name, q, w) for q in range(N) if q != r])
+
+    def fold16(out, lhs, src):
+        for c in range(16):
+            mm(out, a(lhs, 16 - c, 144 - c), src(c), c == 0, c == 15)
+
+    for k, name, w, base in ((0, "xw", C, G0), (1, "land1", 3, 0), (2, "ftab", C, G0), (3, "land2", 3, 0), (4, "xm", C, 0),
+                             (5, "st", C, G0), (6, "numt", C, G0)):
+        arrive(k, name, w, base)
+
+    dma("y", a("wr", p1=8), lambda: T.w[:, :])
+    dma("s", a("bli"), lambda: T.bl[:, :])
+    dma("y", a("nbi"), lambda: T.nb[:, :])
+    dma("s", a("xw", SH, G0), lambda: T.x[:, :])
+    for c in range(16):
+        dma("y", a("wa", 0, 2 * V, p0=c, ps=16), lambda: T.w[:, 0:2 * V])
+    dma("y", a("xo"), lambda: T.x[:, :])
+    iota(a("pf"), [[1, 1]], 0, 1)
+    iota(a("jj"), [[1, 144]], -16, 0)
+    iota(a("pi"), [[1, 1]], 0, 1)
+    iota(a("cols"), [[1, 16]], 0, 0)
+    iota(a("gid", SH, G0), [[1, V]], 0, 0)
+    iota(a("jm"), [[16, 8], [0, 16]], 0, 0)
+    iota(a("v16"), [[16, 128]], 0, 0)
+    iota(a("basec"), [[50, 8], [0, 3]], 1 - (SH + V + C * r - 1024), 0)
+    ts(a("idb"), a("jj", 16, 144), a("pf"), Op.is_equal)
+    ts(a("ci"), a("pi"), 15, Op.bitwise_and)
+    ts(a("ip"), a("jj", 16, 144), a("pf"), Op.is_equal, 4096.0, Op.mult)
+    tc(a("cf"), a("ci"))
+    ts(a("inn"), a("jj", 16, 144), a("pf"), Op.is_equal, -4096.0, Op.mult)
+    tt(a("p16"), a("pf"), a("cf"), Op.subtract)
+    ts(a("mc"), a("cols"), a("cf"), Op.is_equal)
+    ts(a("gsh"), a("jj"), a("p16"), Op.is_equal)
+    ts(a("bll"), a("bli"), 15, Op.bitwise_and)
+    ts(a("blh"), a("bli"), 4, Op.logical_shift_right)
+    tc(a("blu"), a("bli"))
+    tc(a("blo"), a("bll"))
+    tc(a("blx"), a("blh"))
+    ms(a("xw", 0, SH), 0.0)
+    for d in range(D):
+        ts(a("nbc", 128 * d, 128 * d + 128), a("nbi", 128 * d, 128 * d + 128), float(SH + (3 - d) * 4096), Op.add)
+    for d in range(D):
+        for c in range(16):
+            mm(a("k%d" % (d // 2), 128 * (d % 2) + c, 128 * (d % 2) + 128, 16),
+               a("wr", V * d + c, V * d + V, 16, p1=8), a("idb", 0, 8, p1=8))
+    act(a("mask"), ind(a("mc"), a("blo")))
+    act(a("wT", 0, 256), a("k0", 0, 256))
+    act(a("wT", 256, 384), a("k1", 0, 128))
+    act(a("gidb"), ind(a("gid", SH, G0), a("blu")))
+    act(a("xb"), ind(a("xw", SH, G0), a("blu")))
+    send(0, "xb", C, "xw", G0)
+
+    ms(a("od"), float(BIG))
+    ms(a("gid", 0, SH), float(BIG))
+    tt(a("gt", 256, 384), a("k0", 128, 256), a("wT", 0, 128), Op.is_gt)
+    tt(a("gt", 0, 256), a("k1", 0, 256), a("wT", 0, 256), Op.is_gt)
+    tt(a("gt", 512, 640), a("k1", 128, 256), a("wT", 0, 128), Op.is_gt)
+    tt(a("gt", 640, 768), a("k1", 0, 128), a("wT", 128, 256), Op.is_gt)
+    tt(a("gt", 384, 512), a("k1", 128, 256), a("wT", 256, 384), Op.is_gt)
+    g02, g13, g01, g23, g03, g12 = [a("gt", 128 * i, 128 * i + 128) for i in range(6)]
+    for d, terms in enumerate((((g01, -1), (g02, -1), (g03, -1)), ((g01, 1), (g13, -1), (g12, -1)),
+                               ((g02, 1), (g12, 1), (g23, -1)), ((g13, 1), (g03, 1), (g23, 1)))):
+        for i, (s, sg) in enumerate(terms):
+            mm(a("k2", 128 * d, 128 * d + 128), s, a("ip" if sg > 0 else "inn"), i == 0, i == 2)
+    if r > 0:
+        ms(a("gid", G0, G0 + C * r), -1.0)
+    if r < 7:
+        ms(a("gid", G0 + C * r + C, TB), float(BIG))
+    ms(a("ptab1", 0, SH), float(BIG))
+    act(slot("gid", r, C, G0), slot("gidb", r, C))
+    for q in range(N):
+        act(a("od", 50 * q + 1, 50 * q + 49), slot("gidb", q, C))
+    act(slot("xw", r, C, G0), slot("xb", r, C))
+    tt(a("code"), a("k2"), a("nbc"), Op.add)
+    tt(a("h1"), a("code", 0, 256), a("code", 256, 512), Op.max)
+    tt(a("q1"), a("h1", 0, 128), a("h1", 128, 256), Op.max)
+    ts(a("l1i"), a("q1"), 4095, Op.bitwise_and)
+    ts(a("l1s"), a("l1i"), -1024.0, Op.add)
+    tc(a("l1u"), a("l1i"))
+    tt(a("lm"), ind(a("l1s"), a("blx")), a("mask"), Op.mult)
+    fold16(a("k3", 0, 24), "gsh", lambda c: a("lm", c, NG, 16))
+    ms(a("ftab", 0, SH), 0.0)
+    ts(a("gsf"), a("jj"), a("p16"), Op.is_equal)
+    tc(a("l1b"), a("k3", 0, 24))
+    send(1, "l1b", 3, "land1")
+    dma("y", slot("land1", r, 3), slot("l1b", r, 3))
+    ts(a("l1bu"), a("l1b"), 1024.0, Op.add)
+    ts(a("se1", 0, 3), slot("l1b", r, 3), 1024.0, Op.add)
+
+    act(a("ptab1", SH, G0), ind(a("gid"), a("l1u")))
+    for d in range(D):
+        tt(a("cmk", NG * d, NG * d + NG), ind(a("code", 128 * d, 128 * d + 128), a("blx")), a("mask"), Op.mult)
+    fold16(a("k3", 0, 96), "gsf", lambda c: a("cmk", c, 1536, 16))
+    ts(a("c1000"), a("cf"), 1000.0, Op.mult)
+    ts(a("nbu"), a("nbi"), float(SH), Op.add)
+    tt(a("pX"), a("c1000"), a("pf"), Op.add)
+    ts(a("pE"), a("pf"), 16.0, Op.mult)
+    ts(a("hb"), a("jj"), a("pX"), Op.is_equal)
+    ts(a("e16"), a("jm"), a("pE"), Op.is_equal)
+    ts(a("gb"), a("jm"), a("p16"), Op.is_equal)
+    ts(a("tri0"), a("jj", 16, 144), a("pf"), Op.is_lt, -1.0, Op.mult)
+    ms(a("zz"), 0.0)
+    tt(a("tri"), a("tri0"), a("gb"), Op.mult)
+    for d in (0, 1):
+        act(a("wb", NG * d, NG * d + NG), ind(a("wa", V * d, V * d + V), a("blu")))
+    act(a("yw", V, 2 * V), a("gid", SH, G0), scale=0.0)
+
+    def decode(land, dd, lu, se, ptab):
+        c = SH + V + C * r - 1024
+        ts(a(dd), a(land), float(c - 1), Op.max, float(c + C), Op.min)
+        tt(a(lu), a(dd), a("basec"), Op.add)
+        tc(a(ptab, G0, TB), ind(a("od"), a(lu)))
+        tc(slot(ptab, r, C, G0), ind(a("gid"), a(se, 0, 3)))
+
+    def wcast(buf, d, c0):
+        mm(a(buf), a("e16", p1=8), a("wr", V * d + c0, V * d + c0 + 512, p1=8))
+
+    decode("land1", "d1", "lu1", "se1", "ptab1")
+    tt(a("f1b"), ind(a("ptab1"), a("l1bu")), a("gidb"), Op.not_equal)
+    send(2, "f1b", C, "ftab", G0)
+    act(slot("ftab", r, C, G0), slot("f1b", r, C))
+    tt(a("ftab", SH, G0), ind(a("ptab1"), a("l1u")), a("gid", SH, G0), Op.not_equal)
+    tc(a("codeb"), a("k3", 0, 96))
+    ts(a("m1b"), a("f1b"), -1.0, Op.mult, 1.0, Op.add)
+    tc(a("nbbi"), a("codeb"))
+    tt(a("z1b"), ind(a("xw"), a("l1bu")), a("m1b"), Op.mult)
+    ts(a("nbba"), a("nbbi"), 4095, Op.bitwise_and)
+    tc(a("nbbu"), a("nbba"))
+    for i in range(8):
+        wcast("k%d" % (4 + i % 4), 2 + i // 4, 512 * (i % 4))
+        act(a("wa", 2 * V + 512 * i, 2 * V + 512 * i + 512), a("k%d" % (4 + i % 4)))
+
+    act(a("fb", 0, 768), ind(a("ftab"), a("nbbu", 0, 48)))
+    tc(a("fb", 768, 1536), ind(a("ftab"), a("nbbu", 48, 96)))
+    fold16(a("k1", 0, 96), "hb", lambda c: a("fb", c, 1536, 16))
+    for d in (0, 1):
+        act(a("fl", V * d, V * d + V), ind(a("ftab"), a("nbu", 128 * d, 128 * d + 128)))
+    ms(a("ptab2", 0, SH), float(BIG))
+    ts(a("hh"), a("jj"), a("pX"), Op.is_equal)
+    ts(a("hf"), a("jj"), a("pX"), Op.is_equal)
+    ts(a("idf"), a("jj", 16, 144), a("pf"), Op.is_equal)
+    tt(a("kb"), a("codeb"), a("k1", 0, 96), Op.mult)
+    tt(a("h2b"), a("kb", 0, 48), a("kb", 48, 96), Op.max)
+    tt(a("q2b"), a("h2b", 0, 24), a("h2b", 24, 48), Op.max)
+    ts(a("l2bi"), a("q2b"), 4095, Op.bitwise_and)
+    ts(a("l2b"), a("l2bi"), -1024.0, Op.add)
+    send(3, "l2b", 3, "land2")
+    dma("y", slot("land2", r, 3), slot("l2b", r, 3))
+    tc(a("l2bu"), a("l2bi"))
+    ts(a("se2", 0, 3), slot("l2b", r, 3), 1024.0, Op.add)
+    act(a("fl", 2 * V, 2 * V + 768), ind(a("ftab"), a("nbu", 256, 304)))
+    tc(a("fl", 2 * V + 768, 3 * V), ind(a("ftab"), a("nbu", 304, 384)))
+    tc(a("fl", 3 * V, 4 * V), ind(a("ftab"), a("nbu", 384, 512)))
+    for d in range(D):
+        fold16(a("k2", 128 * d, 128 * d + 128), "hb", lambda c: a("fl", V * d + c, V * d + V, 16))
+    act(a("y2b"), ind(a("xw"), a("l2bu")))
+    act(a("k4", 0, NG), a("y2b"))
+    act(a("k5", 0, NG), a("z1b"))
+    decode("land2", "d2", "lu2", "se2", "ptab2")
+    tt(a("key"), a("code"), a("k2"), Op.mult)
+    tt(a("h2"), a("key", 0, 256), a("key", 256, 512), Op.max)
+    tt(a("q2"), a("h2", 0, 128), a("h2", 128, 256), Op.max)
+    ts(a("l2i"), a("q2"), 4095, Op.bitwise_and)
+    tc(a("l2u"), a("l2i"))
+    act(a("ptab2", SH, SH + 1024), ind(a("gid"), a("l2u", 0, 64)))
+    tc(a("ptab2", SH + 1024, G0), ind(a("gid"), a("l2u", 64, 128)))
+    tt(a("m2b"), ind(a("ptab2"), a("l2bu")), a("gidb"), Op.is_equal)
+    tt(a("t2b"), a("m2b"), a("k4", 0, NG), Op.mult)
+    tt(a("xmb"), a("t2b"), a("k5", 0, NG), Op.add)
+    send(4, "xmb", C, "xm")
+    act(a("pp2", 0, 1024), ind(a("ptab2"), a("l2u", 0, 64)))
+    tc(a("pp2", 1024, 2048), ind(a("ptab2"), a("l2u", 64, 128)))
+    for d in (2, 3):
+        act(a("wb", NG * d, NG * d + NG), ind(a("wa", V * d, V * d + V), a("blu")))
+    for c in range(16):
+        act(a("rm", 128 * c, 128 * c + 128), a("gb"), scale=a("mc", c, c + 1))
+    fold16(a("k3", 0, 128), "hb", lambda c: a("ftab", SH + c, G0, 16))
+    fold16(a("k0", 0, 128), "hh", lambda c: a("pp2", c, 2048, 16))
+    ts(a("vB"), a("v16"), a("cf"), Op.add)
+    ts(a("m1B"), a("k3", 0, 128), -1.0, Op.mult, 1.0, Op.add)
+    tc(a("l1f"), a("l1i"))
+    tc(a("l2f"), a("l2i"))
+    tt(a("l1m"), a("m1B"), a("l1f"), Op.mult)
+    tt(a("m2B"), a("k0", 0, 128), a("vB"), Op.is_equal)
+    tt(a("m2l"), a("m2B"), a("l2f"), Op.mult)
+    tt(a("mu"), a("m2l"), a("l1m"), Op.max)
+    tt(a("xt", SH, G0), ind(a("xw"), a("mu")), a("xo"), Op.add)
+    act(slot("xm", r, C), slot("xmb", r, C))
+    act(a("mg"), ind(a("gid"), a("mu")))
+    for d in (2, 3):
+        mm(a("k%d" % (4 + d), 0, NG), a("idb"), a("wb", NG * d, NG * d + NG))
+    mm(a("k1", 0, NG), a("idb"), a("xw", G0, TB), True, False)
+    mm(a("k1", 0, NG), a("idb"), a("xm"), False, True)
+    act(a("xt", G0, TB), a("k1", 0, NG))
+    wcast("k4", 2, 0)
+    wcast("k5", 3, 0)
+    fold16(a("k3", 0, 128), "hh", lambda c: a("mg", c, 2048, 16))
+    ms(a("xt", 0, SH), 0.0)
+    ms(a("st", 0, SH), 0.0)
+    act(a("cmk", 0, 768), ind(a("xt"), a("nbbu", 48, 96)))
+    tt(a("cmk", 768, 1536), ind(a("xt"), a("nbbu", 0, 48)), a("wb", 0, 768), Op.mult)
+    tt(a("k6", 0, NG), a("cmk", 0, NG), a("k6", 0, NG), Op.mult)
+    tt(a("qb"), a("cmk", NG, 768), a("k7", 0, NG), Op.mult)
+    tt(a("k6", 0, NG), a("cmk", 768, 768 + NG), a("k6", 0, NG), Op.add)
+    tt(a("k6", 0, NG), a("qb"), a("k6", 0, NG), Op.add)
+    tt(a("sb"), a("cmk", 768 + NG, 1536), a("k6", 0, NG), Op.add)
+    send(5, "sb", C, "st", G0)
+    wcast("k6", 2, 512)
+    wcast("k7", 3, 512)
+
+    def gather23(i):
+        for d, b in ((2, "g2"), (3, "g3")):
+            act(a(b, 512 * i, 512 * i + 512), ind(a("xt"), a("nbu", 128 * d + 32 * i, 128 * d + 32 * i + 32)))
+
+    def products(i, w2, w3, keep):
+        u, ub = 1024 * (i % 2), "ptab2" if i < 2 else "uu"
+        for d in (0, 1):
+            tt(a(ub, u + 512 * d, u + 512 * d + 512), ind(a("xt"), a("nbu", 128 * d + 32 * i, 128 * d + 32 * i + 32)),
+               a("wa", V * d + 512 * i, V * d + 512 * i + 512), Op.mult)
+        x2, x3 = a("g2", 512 * i, 512 * i + 512), a("g3", 512 * i, 512 * i + 512)
+        tt(a(w2) if keep else x2, x2, a(w2), Op.mult)
+        tt(x3, x3, a(w3), Op.mult)
+
+    def sum_v(i, w2):
+        u, ub = 1024 * (i % 2), "ptab2" if i < 2 else "uu"
+        tt(a(w2), a(ub, u, u + 512), a(w2), Op.add)
+        tt(a(w2), a("g3", 512 * i, 512 * i + 512), a(w2), Op.add)
+        tt(a("st", SH + 512 * i, SH + 512 * i + 512), a(ub, u + 512, u + 1024), a(w2), Op.add)
+
+    def sum_t(i, k):
+        u, ub = 1024 * (i % 2), "ptab2" if i < 2 else "uu"
+        xs = (a(ub, u, u + 512), a(ub, u + 512, u + 1024), a("g2", 512 * i, 512 * i + 512), a("g3", 512 * i, 512 * i + 512))
+        for j, x in enumerate(xs):
+            mm(a(k), a("idf"), x, j == 0, j == 3)
+
+    gather23(0)
+    tt(a("rep"), a("k3", 0, 128), a("vB"), Op.is_gt)
+    mm(a("k1", 0, 128), a("gb"), a("rep"))
+    mm(a("k2", 0, 128), a("tri"), a("rep"))
+    op("v", lambda: g.vector.tensor_tensor_scan(ap(a("sc")), ap(a("k1", 0, 128)), ap(a("zz")), 0.0, Op.add, Op.add),
+       [a("sc")], [a("k1", 0, 128), a("zz")])
+    tt(a("nin"), a("sc"), a("k2", 0, 128), Op.add)
+    ts(a("na"), a("nin"), float(BK), Op.add)
+    tt(a("nm"), a("na"), a("rep"), Op.mult)
+    ts(a("numh"), a("nm"), -float(BK + 1), Op.add)
+    products(0, "k4", "k5", False)
+    for b in range(4):
+        for c in range(16):
+            mm(a("k%d" % b, c, 512, 16), a("rm", 128 * c, 128 * c + 128), a("numh", 32 * b, 32 * b + 32))
+    wcast("k4", 2, 1024)
+    wcast("k5", 3, 1024)
+    gather23(1)
+    for b in range(4):
+        act(a("numt", SH + 512 * b, SH + 512 * b + 512), a("k%d" % b), bias=float(V * r))
+    ms(a("numt", 0, SH), -65536.0)
+    sum_t(0, "k0")
+    act(a("numb"), ind(a("numt", SH, G0), a("blu")))
+    act(slot("st", r, C, G0), slot("sb", r, C))
+    act(slot("numt", r, C, G0), slot("numb", r, C))
+    send(6, "numb", C, "numt", G0)
+    products(1, "k6", "k7", False)
+    gather23(2)
+    sum_t(1, "k1")
+    wcast("k6", 2, 1536)
+    wcast("k7", 3, 1536)
+    gather23(3)
+    act(a("st", SH, SH + 512), a("k0"))
+    act(a("st", SH + 512, SH + 1024), a("k1"))
+    products(2, "k4", "k5", True)
+    sum_v(2, "k4")
+    ts(a("po"), a("nm"), float(V - 1 - BK), Op.add)
+    ts(a("numf"), a("nm"), float(V * r - BK - 1), Op.add)
+    tt(a("posu"), a("po"), a("vB"), Op.max)
+    products(3, "k6", "k7", True)
+    sum_v(3, "k6")
+    act(a("ptab1", 0, V), ind(a("numt"), a("mu")))
+    fold16(a("k2", 0, 128), "hf", lambda c: a("ptab1", c, V, 16))
+    cuts = (128, 96, 48, 16, 0)
+    for k1, k0 in zip(cuts, cuts[1:]):
+        act(a("g2", 16 * k0, 16 * k1), ind(a("st"), a("mu", k0, k1)))
+    last = []
+    for i, (k1, k0) in enumerate(zip(cuts, cuts[1:])):
+        if i == 3:
+            tt(a("cmo"), a("k2", 0, 128), a("numf"), Op.max)
+            last.append(dma("y", lambda: T.cm[:, :], a("cmo")))
+        tt(ind(a("yw", 0, V + 16 * k1), a("posu", k0, k1)), a("st", SH + 16 * k0, SH + 16 * k1), a("g2", 16 * k0, 16 * k1), Op.add)
+        last.append(dma("y", (lambda c0, c1: lambda: T.y[:, c0:c1])(16 * k0, 16 * k1), a("yw", V + 16 * k0, V + 16 * k1)))
+    ops.append({"q": "y", "fn": None, "dep": set(last), "inc": 0, "sem": None, "waits": [], "K": 0})
+
+    known = {q: 0 for q in "vstgy"}
+    waiters = {}
+    for i, o in enumerate(ops):
+        if o["q"] == "r":
+            continue
+        k = known[o["q"]]
+        for j in sorted(set(mmgroup.get(j, j) for j in o["dep"]), reverse=True):
+            if not k >> j & 1:
+                k |= ops[j]["K"] | 1 << j
+                o["waits"].append(j)
+                waiters.setdefault(j, []).append(i)
+        known[o["q"]] = o["K"] = k
+    groups = {}
+    for j in sorted(waiters):
+        if ops[j]["q"] != "r":
+            groups.setdefault((ops[j]["q"], tuple(waiters[j])), []).append(j)
+    pool, where, need = [], {}, {}
+    for (q, ws), js in sorted(groups.items(), key=lambda t: t[1][0]):
+        for s, p in enumerate(pool):
+            if p[0] == q and all(all(ops[j]["K"] >> w & 1 or (ops[w]["q"] == q and w < j) for w in p[1]) for j in js):
+                break
+        else:
+            s, p = len(pool), [q, (), 0]
+            pool.append(p)
+        p[1] = ws
+        p[2] += sum(ops[j]["inc"] for j in js)
+        for j in js:
+            where[j], need[j] = "s%d" % s, p[2]
+    assert len(pool) <= NPOOL, len(pool)
+    for i, o in enumerate(ops):
+        if o["q"] == "r":
+            continue
+        w = {}
+        for j in o["waits"]:
+            if ops[j]["q"] == "r":
+                w[ops[j]["sem"]] = ops[j]["inc"]
+            else:
+                w[where[j]] = max(w.get(where[j], 0), need[j])
+        for s in sorted(w):
+            eng[o["q"]].wait_ge(T.sem[s], w[s])
+        if o["fn"] is not None:
+            x = o["fn"]()
+            if i in where:
+                x.then_inc(T.sem[where[i]], o["inc"])
+    g.wait_ge(T.sem["sent"], sent[0])

@@ -7,32 +7,33 @@ SH = 16
 G0 = SH + V
 TB = G0 + NG
 BIG = 4096
-BK = 32768
+PIECES = ((96, 128, 3), (64, 96, 3), (32, 64, 3), (0, 32, 3))
+CUTS = ((128, 96), (96, 64), (64, 32), (32, 12, 0))
 
 _F, _B, _I, _H, _U = "float32", "bfloat16", "int32", "float16", "uint16"
 _LOG = {n: (w, t) for n, w, t in [
-    ("pf", 1, _F), ("pi", 1, _I), ("ci", 1, _I), ("cf", 1, _F), ("c1000", 1, _F), ("p16", 1, _F), ("pX", 1, _F), ("pE", 1, _F),
-    ("jj", 144, _F), ("jm", 128, _F), ("v16", 128, _F), ("vB", 128, _F), ("basec", 24, _F), ("cols", 16, _F), ("mc", 16, _F),
-    ("idb", 128, _B), ("idf", 128, _F), ("e16", 128, _B), ("ip", 128, _B), ("inn", 128, _B), ("gsh", 144, _H), ("gsf", 144, _F),
-    ("hb", 144, _B), ("hh", 144, _H), ("hf", 144, _F), ("gb", 128, _B), ("tri0", 128, _B), ("tri", 128, _B), ("rm", 2048, _H),
-    ("zz", 128, _F), ("gid", TB, _F), ("od", 400, _F),
-    ("wr", 8192, _B), ("nbi", 512, _I), ("bli", 24, _I), ("xw", TB, _B), ("xo", V, _B), ("wa", 8192, _B),
+    ("pf", 1, _F), ("pi", 1, _I), ("ci", 1, _I), ("cf", 1, _F), ("c1000", 1, _F), ("p16", 1, _F), ("pX", 1, _F), ("pY", 1, _F),
+    ("pZ", 1, _F), ("pS", 1, _F), ("sc1", 1, _F), ("bi1", 1, _F), ("u32", 32, _F), ("ee", 32, _B), ("dm", 48, _B),
+    ("jj", 160, _F), ("jm", 128, _F), ("v16", 128, _F), ("vB", 128, _F), ("basec", 24, _F), ("selfc", 3, _F), ("cols", 16, _F),
+    ("mc", 16, _F), ("idb", 128, _B), ("idf", 128, _F), ("ip", 128, _B), ("inn", 128, _B), ("zsl", 160, _H), ("gsh", 144, _H),
+    ("gsf", 144, _F), ("hb", 144, _B), ("hh", 144, _H), ("hh2", 144, _H), ("gb", 128, _B), ("tri0", 128, _B), ("tri", 128, _B),
+    ("sel", 512, _B), ("zz", 128, _F), ("gid", TB, _F), ("od", 400, _F),
+    ("wr", V, _B), ("w16", V, _B), ("nbi", 512, _I), ("bli", 24, _I), ("xw", TB, _B), ("xo", V, _B), ("wa", 2 * V, _B),
     ("nbu", 512, _U), ("nbc", 512, _F), ("blu", 24, _U), ("blh", 24, _I), ("blx", 24, _U), ("bll", 24, _I), ("blo", 24, _U),
     ("gidb", NG, _F), ("mask", NG, _F), ("xb", NG, _B),
-    ("wT", 384, _F), ("gt", 768, _B), ("code", 512, _F), ("h1", 256, _F), ("q1", 128, _I), ("l1i", 128, _I), ("l1u", 128, _U),
-    ("l1s", 128, _F), ("l1f", 128, _F), ("lm", NG, _H), ("l1b", 24, _F), ("l1bu", 24, _U), ("land1", 24, _F), ("d1", 24, _F),
-    ("lu1", 24, _U), ("se1", 4, _U), ("ptab1", TB, _F), ("f1b", NG, _B), ("m1b", NG, _B), ("z1b", NG, _B), ("ftab", TB, _B),
-    ("m1B", 128, _F), ("l1m", 128, _F), ("cmk", 1536, _F), ("codeb", 96, _F), ("nbbi", 96, _I), ("nbba", 96, _I), ("nbbu", 96, _U),
-    ("wb", 1536, _B),
-    ("fb", 1536, _B), ("kb", 96, _F), ("h2b", 48, _F), ("q2b", 24, _I), ("l2bi", 24, _I), ("l2b", 24, _F), ("l2bu", 24, _U),
-    ("fl", 8192, _B), ("key", 512, _F), ("h2", 256, _F), ("q2", 128, _I), ("l2i", 128, _I), ("l2u", 128, _U), ("l2f", 128, _F),
+    ("gt", 768, _B), ("code", 512, _F), ("cs", 512, _I), ("lo", 256, _I), ("q1", 128, _F), ("l1u", 128, _U), ("n3i", 384, _I),
+    ("n3u", 384, _U), ("l1s", 128, _F), ("l1f", 128, _F), ("lm", NG, _H), ("l1b", 24, _F), ("l1bu", 24, _U), ("land1", 24, _F),
+    ("d1", 24, _F), ("lu1", 24, _U), ("se1", 4, _U), ("ptab1", TB, _F), ("ftab", TB, _B), ("m1B", 128, _F), ("l1m", 128, _F),
+    ("cmk", 1536, _F), ("codeb", 96, _I), ("nbba", 96, _I), ("nbbu", 96, _U), ("wb", NG, _B), ("gq", NG, _F),
+    ("fb", 5 * NG, _B), ("kb", 96, _F), ("h2b", 48, _F), ("q2b", 24, _I), ("l2bi", 24, _I), ("l2b", 24, _F), ("l2bu", 24, _U),
+    ("m1bl", 24, _F), ("l1mb", 24, _F), ("candu", 24, _U), ("yc", NG, _B),
+    ("fl", 3 * V, _B), ("key", 384, _F), ("h2", 256, _F), ("q2", 128, _I), ("l2i", 128, _I), ("l2u", 128, _U),
     ("land2", 24, _F), ("d2", 24, _F), ("lu2", 24, _U), ("se2", 4, _U), ("ptab2", TB, _F),
-    ("m2b", NG, _B), ("y2b", NG, _B), ("t2b", NG, _B), ("xmb", NG, _B), ("xm", NG, _B),
-    ("pp2", 2048, _H), ("m2B", 128, _F), ("m2l", 128, _F), ("mu", 128, _U),
-    ("mg", 2048, _H), ("rep", 128, _B), ("sc", 128, _F), ("nin", 128, _F), ("na", 128, _F), ("nm", 128, _F), ("numh", 128, _H),
-    ("numf", 128, _F), ("po", 128, _F), ("posu", 128, _U), ("numt", TB, _F), ("numb", NG, _F), ("cmo", 128, _F),
-    ("xt", TB, _F), ("qb", NG, _F), ("sb", NG, _F), ("st", TB, _F),
-    ("g2", 2048, _F), ("g3", 2048, _F), ("uu", 2048, _F), ("yw", 4096, _F),
+    ("m2b", NG, _B), ("xmb", NG, _B), ("xm", NG, _B),
+    ("pp2", V, _H), ("m2B", 128, _F), ("m2l", 128, _F), ("mu", 128, _U), ("mur", 128, _U),
+    ("mg", V, _H), ("rep", 128, _B), ("sc", 128, _F), ("nin", 128, _H), ("na", 128, _F), ("nm", 128, _F),
+    ("numf", 128, _F), ("posu", 128, _U), ("numt", TB, _F), ("numb", NG, _F), ("nmate", V, _H), ("cmo", 128, _F),
+    ("xt", TB, _F), ("sb", NG, _F), ("st", TB, _F), ("pr", 4 * V, _F), ("g2", V, _F), ("yw", 2 * V, _F),
 ]}
 _WHERE, SCRATCH, _fill = {}, {}, {}
 for _n, (_w, _t) in _LOG.items():
@@ -49,8 +50,8 @@ for _n, _w in _PSUM.items():
     SCRATCH[_n] = ("psum", [128, _w], _F)
     _WHERE[_n] = (_n, 0)
     _LOG[_n] = (_w, _F)
-NPOOL = 120
-SEMAPHORES = ["e%d" % k for k in range(7)] + ["sent"] + ["s%d" % i for i in range(NPOOL)]
+NPOOL = 130
+SEMAPHORES = ["e%d" % k for k in range(7)] + ["t%d" % k for k in range(7)] + ["s%d" % i for i in range(NPOOL)]
 
 
 def a(name, c0=0, c1=None, cs=1, p0=0, p1=128, ps=1):
@@ -110,7 +111,7 @@ def rank_program(g, core, T, topo):
                 out += [s[1], s[2]] if s[0] == "ind" else [s]
         return out
 
-    def op(q, fn, outs, ins, inc=1, stop=None):
+    def op(q, fn, outs, ins, inc=1, stop=None, after=()):
         i = len(ops)
         wr, rd = [], regs(ins)
         for o in outs:
@@ -119,7 +120,7 @@ def rank_program(g, core, T, topo):
                 rd.append(o[2])
             else:
                 wr.append(o)
-        dep = set()
+        dep = set(after)
         for lst, w in ((rd, False), (wr, True)):
             for s in lst:
                 for j, jw, t in acc.get(s[0], ()):
@@ -155,13 +156,15 @@ def rank_program(g, core, T, topo):
     def ms(out, c):
         op("v", lambda: g.vector.memset(ap(out), c), [out], [])
 
-    def act(out, x, scale=None, bias=None):
-        if scale is not None:
+    def act(out, x, scale=1.0, bias=None):
+        if bias is None:
             op("s", lambda: g.scalar.activation(out=ap(out), in_=ap(x), func=Fn.Copy, scale=ap(scale)), [out], [x, scale])
-        elif bias is not None:
-            op("s", lambda: g.scalar.activation(out=ap(out), in_=ap(x), func=Fn.Identity, bias=bias), [out], [x])
         else:
-            op("s", lambda: g.scalar.activation(out=ap(out), in_=ap(x), func=Fn.Copy), [out], [x])
+            op("s", lambda: g.scalar.activation(out=ap(out), in_=ap(x), func=Fn.Identity, bias=ap(bias), scale=ap(scale)),
+               [out], [x, scale, bias])
+
+    def gather(q, out, win, off):
+        (tc if q == "v" else act)(out, ind(win, off))
 
     def mm(out, l, rr, start=True, stop=True):
         op("t", lambda: g.tensor.matmul(ap(out), ap(l), ap(rr), start, stop), [out], [l, rr], stop=stop)
@@ -172,25 +175,29 @@ def rank_program(g, core, T, topo):
         else:
             op("g", lambda: g.iota(ap(out), pattern, base, cm), [out], [])
 
-    def dma(q, out, x):
+    def dma(q, out, x, after=()):
         f = lambda s: ap(s) if isinstance(s, tuple) else s()
-        return op(q, lambda: eng[q].dma_start(out=f(out), in_=f(x)), [out] if isinstance(out, tuple) else [], regs([x]), inc=16)
+        return op(q, lambda: eng[q].dma_start(out=f(out), in_=f(x)), [out] if isinstance(out, tuple) else [], regs([x]), inc=16,
+                  after=after)
 
     plan = _plan(core, topo, T.cores)
     expect = sum(len(_plan(c, topo, T.cores)[core]) for c in T.cores if c != core)
-    sent = [0]
+    engines = sum(len(e) for e in plan.values())
 
     def slot(name, q, w, base=0):
         return a(name, base + w * q, base + w * q + w)
 
+    def event(sem, count):
+        ops.append({"q": "r", "fn": None, "dep": set(), "inc": count, "sem": sem, "waits": [], "K": 0})
+        return len(ops) - 1
+
     def arrive(k, name, w, base=0):
-        i = len(ops)
         for q in range(N):
             if q != r:
-                acc.setdefault(name, []).append((i, True, slot(name, q, w, base)))
-        ops.append({"q": "r", "fn": None, "dep": set(), "inc": expect, "sem": "e%d" % k, "waits": [], "K": 0})
+                acc.setdefault(name, []).append((len(ops), True, slot(name, q, w, base)))
+        event("e%d" % k, expect)
 
-    def send(k, name, w, dname, base=0):
+    def send(k, name, w, dname, base=0, sbase=0):
         dst = slot(dname, r, w, base)
 
         def fn():
@@ -199,296 +206,377 @@ def rank_program(g, core, T, topo):
                 if q != r:
                     rid, pid, _se = topo.addr(T.cores[q])
                     tr.append(RemoteDMATransfer(dst_ids=[DstId(rid=rid, pnc=pid)], dma_engine_mask=sum(1 << e for e in plan[T.cores[q]]),
-                                                remote_sem=T.sem["e%d" % k], src=ap(slot(name, q, w)), dst=ap(dst)))
-            g.remote_dma_fused(tr, local_sem=T.sem["sent"])
-            sent[0] += sum(len(e) for e in plan.values())
-        op("g", fn, [], [slot(name, q, w) for q in range(N) if q != r])
+                                                remote_sem=T.sem["e%d" % k], src=ap(slot(name, q, w, sbase)), dst=ap(dst)))
+            g.remote_dma_fused(tr, local_sem=T.sem["t%d" % k])
+        op("g", fn, [], [slot(name, q, w, sbase) for q in range(N) if q != r])
+        return event("t%d" % k, engines)
 
-    def fold16(out, lhs, src):
+    def fold16(out, lhs, name, c0, c1):
         for c in range(16):
-            mm(out, a(lhs, 16 - c, 144 - c), src(c), c == 0, c == 15)
+            mm(out, a(lhs, 16 - c, 144 - c), a(name, c0 + c, c1, 16), c == 0, c == 15)
 
     for k, name, w, base in ((0, "xw", C, G0), (1, "land1", 3, 0), (2, "ftab", C, G0), (3, "land2", 3, 0), (4, "xm", C, 0),
                              (5, "st", C, G0), (6, "numt", C, G0)):
         arrive(k, name, w, base)
+    me = G0 + C * r
 
-    dma("y", a("wr", p1=8), lambda: T.w[:, :])
+    dma("y", a("wr", p1=32), lambda: T.w[:, :])
     dma("s", a("bli"), lambda: T.bl[:, :])
+    dma("y", a("xw", SH, G0), lambda: T.x[:, :])
     dma("y", a("nbi"), lambda: T.nb[:, :])
-    dma("s", a("xw", SH, G0), lambda: T.x[:, :])
-    for c in range(16):
-        dma("y", a("wa", 0, 2 * V, p0=c, ps=16), lambda: T.w[:, 0:2 * V])
-    dma("y", a("xo"), lambda: T.x[:, :])
+    iota(a("u32"), [[1, 4], [4, 8]], 0, -1)
     iota(a("pf"), [[1, 1]], 0, 1)
-    iota(a("jj"), [[1, 144]], -16, 0)
     iota(a("pi"), [[1, 1]], 0, 1)
-    iota(a("cols"), [[1, 16]], 0, 0)
-    iota(a("gid", SH, G0), [[1, V]], 0, 0)
+    iota(a("jj"), [[1, 160]], -16, 0)
     iota(a("jm"), [[16, 8], [0, 16]], 0, 0)
+    iota(a("gid", SH, SH + 512), [[1, 512]], 0, 0)
     iota(a("v16"), [[16, 128]], 0, 0)
-    iota(a("basec"), [[50, 8], [0, 3]], 1 - (SH + V + C * r - 1024), 0)
-    ts(a("idb"), a("jj", 16, 144), a("pf"), Op.is_equal)
+    iota(a("basec"), [[50, 8], [0, 3]], 1 - me, 0)
+    ms(a("od"), float(BIG))
+    ts(a("ee"), a("u32"), 0.0, Op.is_equal)
+    tt(a("dm", 0, 24), a("ee", 8, 32), a("ee", 0, 24), Op.subtract)
+    tt(a("dm", 24, 40), a("ee", 16, 32), a("ee", 0, 16), Op.subtract)
+    tt(a("dm", 40, 48), a("ee", 24, 32), a("ee", 0, 8), Op.subtract)
     ts(a("ci"), a("pi"), 15, Op.bitwise_and)
-    ts(a("ip"), a("jj", 16, 144), a("pf"), Op.is_equal, 4096.0, Op.mult)
+    ms(a("gid", 0, SH), float(BIG))
     tc(a("cf"), a("ci"))
-    ts(a("inn"), a("jj", 16, 144), a("pf"), Op.is_equal, -4096.0, Op.mult)
+    if r > 0:
+        ms(a("gid", G0, me), -1.0)
+    if r < 7:
+        ms(a("gid", me + C, TB), float(BIG))
+    ts(a("zsl"), a("jj"), a("pf"), Op.is_equal)
+    ts(a("mc"), a("jj", 16, 32), a("cf"), Op.is_equal)
     tt(a("p16"), a("pf"), a("cf"), Op.subtract)
-    ts(a("mc"), a("cols"), a("cf"), Op.is_equal)
-    ts(a("gsh"), a("jj"), a("p16"), Op.is_equal)
+    ts(a("c1000"), a("cf"), 1000.0, Op.mult)
+    act(a("ip"), a("zsl", 16, 144), scale=4096.0)
+    act(a("inn"), a("zsl", 16, 144), scale=-4096.0)
+    act(a("idb"), a("zsl", 16, 144))
+    act(a("idf"), a("zsl", 16, 144))
+    ts(a("gsh"), a("jj", 0, 144), a("p16"), Op.is_equal)
+    tt(a("pX"), a("c1000"), a("pf"), Op.add)
+    ts(a("tri0"), a("jj", 16, 144), a("pf"), Op.is_lt, -1.0, Op.mult)
+    ts(a("hb"), a("jj", 0, 144), a("pX"), Op.is_equal)
     ts(a("bll"), a("bli"), 15, Op.bitwise_and)
     ts(a("blh"), a("bli"), 4, Op.logical_shift_right)
     tc(a("blu"), a("bli"))
     tc(a("blo"), a("bll"))
     tc(a("blx"), a("blh"))
-    ms(a("xw", 0, SH), 0.0)
+    ts(a("gb"), a("jm"), a("p16"), Op.is_equal)
     for d in range(D):
-        ts(a("nbc", 128 * d, 128 * d + 128), a("nbi", 128 * d, 128 * d + 128), float(SH + (3 - d) * 4096), Op.add)
-    for d in range(D):
+        ts(a("sel", 128 * d, 128 * d + 128), a("jm"), float(d), Op.add, a("pf"), Op.is_equal)
+    gather("s", a("mask"), a("mc"), a("blo"))
+    act(a("gid", SH + 512, SH + 1024), a("gid", SH, SH + 512), bias=512.0)
+    for b in (0, 1):
         for c in range(16):
-            mm(a("k%d" % (d // 2), 128 * (d % 2) + c, 128 * (d % 2) + 128, 16),
-               a("wr", V * d + c, V * d + V, 16, p1=8), a("idb", 0, 8, p1=8))
-    act(a("mask"), ind(a("mc"), a("blo")))
-    act(a("wT", 0, 256), a("k0", 0, 256))
-    act(a("wT", 256, 384), a("k1", 0, 128))
-    act(a("gidb"), ind(a("gid", SH, G0), a("blu")))
-    act(a("xb"), ind(a("xw", SH, G0), a("blu")))
+            mm(a("k%d" % b, c, 384, 16), a("wr", c, V, 16, p1=32), a("dm", 24 * b, 24 * b + 24, p1=32))
+    gather("s", a("xb"), a("xw", SH, G0), a("blu"))
     send(0, "xb", C, "xw", G0)
+    act(a("gid", SH + 1024, G0), a("gid", SH, SH + 1024), bias=1024.0)
+    gather("s", a("gidb"), a("gid", SH, G0), a("blu"))
 
-    ms(a("od"), float(BIG))
-    ms(a("gid", 0, SH), float(BIG))
-    tt(a("gt", 256, 384), a("k0", 128, 256), a("wT", 0, 128), Op.is_gt)
-    tt(a("gt", 0, 256), a("k1", 0, 256), a("wT", 0, 256), Op.is_gt)
-    tt(a("gt", 512, 640), a("k1", 128, 256), a("wT", 0, 128), Op.is_gt)
-    tt(a("gt", 640, 768), a("k1", 0, 128), a("wT", 128, 256), Op.is_gt)
-    tt(a("gt", 384, 512), a("k1", 128, 256), a("wT", 256, 384), Op.is_gt)
-    g02, g13, g01, g23, g03, g12 = [a("gt", 128 * i, 128 * i + 128) for i in range(6)]
-    for d, terms in enumerate((((g01, -1), (g02, -1), (g03, -1)), ((g01, 1), (g13, -1), (g12, -1)),
-                               ((g02, 1), (g12, 1), (g23, -1)), ((g13, 1), (g03, 1), (g23, 1)))):
+    ts(a("gt", 0, 384), a("k0", 0, 384), 0.0, Op.is_gt)
+    ts(a("gt", 384, 768), a("k1", 0, 384), 0.0, Op.is_gt)
+    g01, g12, g23, g02, g13, g03 = [a("gt", 128 * i, 128 * i + 128) for i in range(6)]
+    for d, terms in enumerate((((g01, -1), (g02, -1), (g03, -1)), ((g01, 1), (g12, -1), (g13, -1)),
+                               ((g12, 1), (g23, -1), (g02, 1)), ((g23, 1), (g13, 1), (g03, 1)))):
         for i, (s, sg) in enumerate(terms):
             mm(a("k2", 128 * d, 128 * d + 128), s, a("ip" if sg > 0 else "inn"), i == 0, i == 2)
-    if r > 0:
-        ms(a("gid", G0, G0 + C * r), -1.0)
-    if r < 7:
-        ms(a("gid", G0 + C * r + C, TB), float(BIG))
-    ms(a("ptab1", 0, SH), float(BIG))
+    ts(a("vB"), a("v16"), a("cf"), Op.add)
+    ts(a("selfc"), a("v16", 0, 3), a("cf"), Op.add, float(me), Op.add)
+    for land in ("land1", "land2"):
+        dma("y", slot(land, r, 3), a("selfc"))
+    tt(a("tri"), a("tri0"), a("gb"), Op.mult)
+    for d in range(D):
+        ts(a("nbc", 128 * d, 128 * d + 128), a("nbi", 128 * d, 128 * d + 128), float(SH + (3 - d) * 4096), Op.add)
     act(slot("gid", r, C, G0), slot("gidb", r, C))
-    for q in range(N):
-        act(a("od", 50 * q + 1, 50 * q + 49), slot("gidb", q, C))
-    act(slot("xw", r, C, G0), slot("xb", r, C))
+    act(a("gsf"), a("gsh"))
+    act(a("hh"), a("hb"))
     tt(a("code"), a("k2"), a("nbc"), Op.add)
-    tt(a("h1"), a("code", 0, 256), a("code", 256, 512), Op.max)
-    tt(a("q1"), a("h1", 0, 128), a("h1", 128, 256), Op.max)
-    ts(a("l1i"), a("q1"), 4095, Op.bitwise_and)
-    ts(a("l1s"), a("l1i"), -1024.0, Op.add)
-    tc(a("l1u"), a("l1i"))
+    tt(a("cs", 0, 256), a("code", 0, 256), a("code", 256, 512), Op.max)
+    tt(a("q1"), a("cs", 0, 128), a("cs", 128, 256), Op.max)
+    ts(a("l1s"), a("q1"), -float(3 * 4096 + 1024), Op.add)
+    ts(a("l1u"), a("q1"), -float(3 * 4096), Op.add)
     tt(a("lm"), ind(a("l1s"), a("blx")), a("mask"), Op.mult)
-    fold16(a("k3", 0, 24), "gsh", lambda c: a("lm", c, NG, 16))
-    ms(a("ftab", 0, SH), 0.0)
-    ts(a("gsf"), a("jj"), a("p16"), Op.is_equal)
-    tc(a("l1b"), a("k3", 0, 24))
-    send(1, "l1b", 3, "land1")
-    dma("y", slot("land1", r, 3), slot("l1b", r, 3))
-    ts(a("l1bu"), a("l1b"), 1024.0, Op.add)
-    ts(a("se1", 0, 3), slot("l1b", r, 3), 1024.0, Op.add)
+    fold16(a("k3", 0, 24), "gsh", "lm", 0, NG)
+    gather("s", a("ptab1", SH, G0), a("gid"), a("l1u"))
+    tt(a("lo"), a("code", 0, 256), a("code", 256, 512), Op.min)
+    ts(a("l1b"), a("k3", 0, 24), 1024.0, Op.add)
+    left1 = send(1, "l1b", 3, "land1")
+    iota(a("yw", V, V + 1024), [[0, 1024]], 0, 0)
+    for c in range(16):
+        dma("y", a("w16", p0=c, ps=16), (lambda d: lambda: T.w[:, V * d:V * d + V])(c % D), after=[left1])
 
-    act(a("ptab1", SH, G0), ind(a("gid"), a("l1u")))
+    tc(a("l1bu"), a("l1b"))
+    tc(a("se1", 0, 3), slot("l1b", r, 3))
+    ms(a("ptab1", 0, SH), float(BIG))
     for d in range(D):
         tt(a("cmk", NG * d, NG * d + NG), ind(a("code", 128 * d, 128 * d + 128), a("blx")), a("mask"), Op.mult)
-    fold16(a("k3", 0, 96), "gsf", lambda c: a("cmk", c, 1536, 16))
-    ts(a("c1000"), a("cf"), 1000.0, Op.mult)
-    ts(a("nbu"), a("nbi"), float(SH), Op.add)
-    tt(a("pX"), a("c1000"), a("pf"), Op.add)
-    ts(a("pE"), a("pf"), 16.0, Op.mult)
-    ts(a("hb"), a("jj"), a("pX"), Op.is_equal)
-    ts(a("e16"), a("jm"), a("pE"), Op.is_equal)
-    ts(a("gb"), a("jm"), a("p16"), Op.is_equal)
-    ts(a("tri0"), a("jj", 16, 144), a("pf"), Op.is_lt, -1.0, Op.mult)
-    ms(a("zz"), 0.0)
-    tt(a("tri"), a("tri0"), a("gb"), Op.mult)
-    for d in (0, 1):
-        act(a("wb", NG * d, NG * d + NG), ind(a("wa", V * d, V * d + V), a("blu")))
-    act(a("yw", V, 2 * V), a("gid", SH, G0), scale=0.0)
-
-    def decode(land, dd, lu, se, ptab):
-        c = SH + V + C * r - 1024
-        ts(a(dd), a(land), float(c - 1), Op.max, float(c + C), Op.min)
-        tt(a(lu), a(dd), a("basec"), Op.add)
-        tc(a(ptab, G0, TB), ind(a("od"), a(lu)))
-        tc(slot(ptab, r, C, G0), ind(a("gid"), a(se, 0, 3)))
-
-    def wcast(buf, d, c0):
-        mm(a(buf), a("e16", p1=8), a("wr", V * d + c0, V * d + c0 + 512, p1=8))
-
-    decode("land1", "d1", "lu1", "se1", "ptab1")
-    tt(a("f1b"), ind(a("ptab1"), a("l1bu")), a("gidb"), Op.not_equal)
-    send(2, "f1b", C, "ftab", G0)
-    act(slot("ftab", r, C, G0), slot("f1b", r, C))
-    tt(a("ftab", SH, G0), ind(a("ptab1"), a("l1u")), a("gid", SH, G0), Op.not_equal)
-    tc(a("codeb"), a("k3", 0, 96))
-    ts(a("m1b"), a("f1b"), -1.0, Op.mult, 1.0, Op.add)
-    tc(a("nbbi"), a("codeb"))
-    tt(a("z1b"), ind(a("xw"), a("l1bu")), a("m1b"), Op.mult)
-    ts(a("nbba"), a("nbbi"), 4095, Op.bitwise_and)
-    tc(a("nbbu"), a("nbba"))
-    for i in range(8):
-        wcast("k%d" % (4 + i % 4), 2 + i // 4, 512 * (i % 4))
-        act(a("wa", 2 * V + 512 * i, 2 * V + 512 * i + 512), a("k%d" % (4 + i % 4)))
-
-    act(a("fb", 0, 768), ind(a("ftab"), a("nbbu", 0, 48)))
-    tc(a("fb", 768, 1536), ind(a("ftab"), a("nbbu", 48, 96)))
-    fold16(a("k1", 0, 96), "hb", lambda c: a("fb", c, 1536, 16))
-    for d in (0, 1):
-        act(a("fl", V * d, V * d + V), ind(a("ftab"), a("nbu", 128 * d, 128 * d + 128)))
+    for name in ("xw", "ftab", "xt", "st"):
+        ms(a(name, 0, SH), 0.0)
     ms(a("ptab2", 0, SH), float(BIG))
-    ts(a("hh"), a("jj"), a("pX"), Op.is_equal)
-    ts(a("hf"), a("jj"), a("pX"), Op.is_equal)
-    ts(a("idf"), a("jj", 16, 144), a("pf"), Op.is_equal)
+    for q in range(N):
+        if q != r:
+            act(a("od", 50 * q + 1, 50 * q + 49), slot("gidb", q, C))
+    gather("s", a("od", 50 * r + 1, 50 * r + 49), a("gid"), a("se1", 0, 3))
+    act(slot("xw", r, C, G0), slot("xb", r, C))
+    act(a("l1f"), a("q1"), bias=-float(3 * 4096))
+    for d in range(D):
+        act(a("nbu", 128 * d, 128 * d + 128), a("nbc", 128 * d, 128 * d + 128), bias=-float((3 - d) * 4096))
+    act(a("zz"), a("jm"), scale=0.0)
+    for k0, k1, t in PIECES[:-1]:
+        act(a("st", 8 + 16 * k0, SH + 16 * k0), a("jm", 0, 8), scale=0.0)
+    act(a("numt", 0, SH), a("jm", 0, SH), scale=0.0, bias=64.0)
+    fold16(a("k4", 0, 96), "gsf", "cmk", 0, 1536)
+
+    def decode(q, land, dd, lu, ptab):
+        ts(a(dd), a(land), float(me - 1), Op.max, float(me + C), Op.min)
+        tt(a(lu), a(dd), a("basec"), Op.add)
+        gather(q, a(ptab, G0, TB), a("od"), a(lu))
+
+    decode("s", "land1", "d1", "lu1", "ptab1")
+    tt(a("cs", 256, 384), a("lo", 0, 128), a("lo", 128, 256), Op.max)
+    tt(a("cs", 384, 512), a("lo", 0, 128), a("lo", 128, 256), Op.min)
+    f1b = a("fb", 4 * NG, 5 * NG)
+    tt(f1b, ind(a("ptab1"), a("l1bu")), a("gidb"), Op.not_equal)
+    left2 = send(2, "fb", C, "ftab", G0, 4 * NG)
+    iota(a("yw", V + 1024, 2 * V), [[0, 1024]], 0, 0)
+    dma("y", a("xo"), lambda: T.x[:, :], after=[left2])
+    act(slot("ftab", r, C, G0), slot("fb", r, C, 4 * NG))
+    act(a("k5", 0, NG), f1b, scale=-float(BIG), bias=float(BIG))
+    ts(a("n3i"), a("cs", 0, 384), 4095, Op.bitwise_and)
+    tc(a("codeb"), a("k4", 0, 96))
+    act(a("n3u"), a("n3i"))
+    gather("s", a("wb"), a("w16"), a("blu"))
+    tt(a("ftab", SH, G0), ind(a("ptab1"), a("l1u")), a("gid", SH, G0), Op.not_equal)
+    fold16(a("k0", 0, 128), "hb", "ftab", SH, G0)
+    ts(a("nbba"), a("codeb"), 4095, Op.bitwise_and)
+    act(a("sc1"), a("mc", 1, 2), scale=-1.0, bias=1.0)
+    act(a("bi1"), a("mc", 1, 2), scale=float(r + 1), bias=-1.0)
+    act(a("pS"), a("cf"), scale=2047.0, bias=1.0)
+    tc(a("nbbu"), a("nbba"))
+    tt(a("gq"), a("gidb"), a("k5", 0, NG), Op.max)
+
+    gather("s", a("fb", 0, 768), a("ftab"), a("nbbu", 0, 48))
+    gather("v", a("fb", 768, 1536), a("ftab"), a("nbbu", 48, 96))
+    fold16(a("k1", 0, 120), "hb", "fb", 0, 5 * NG)
+
+    def flags(q, d, h, k0=0, k1=64):
+        c, k = 1024 * (2 * d + h), 128 * d + 64 * h
+        gather(q, a("fl", c + 16 * k0, c + 16 * k1), a("ftab"), a("n3u", k + k0, k + k1))
+
+    def flagfold(d, h):
+        c = 1024 * (2 * d + h)
+        fold16(a("k%d" % (2 + h), 64 * d, 64 * d + 64), "hb", "fl", c, c + 1024)
+
+    flags("s", 0, 0)
+    flagfold(0, 0)
+    flags("v", 2, 0)
+    flagfold(2, 0)
     tt(a("kb"), a("codeb"), a("k1", 0, 96), Op.mult)
     tt(a("h2b"), a("kb", 0, 48), a("kb", 48, 96), Op.max)
     tt(a("q2b"), a("h2b", 0, 24), a("h2b", 24, 48), Op.max)
     ts(a("l2bi"), a("q2b"), 4095, Op.bitwise_and)
-    ts(a("l2b"), a("l2bi"), -1024.0, Op.add)
-    send(3, "l2b", 3, "land2")
-    dma("y", slot("land2", r, 3), slot("l2b", r, 3))
-    tc(a("l2bu"), a("l2bi"))
-    ts(a("se2", 0, 3), slot("l2b", r, 3), 1024.0, Op.add)
-    act(a("fl", 2 * V, 2 * V + 768), ind(a("ftab"), a("nbu", 256, 304)))
-    tc(a("fl", 2 * V + 768, 3 * V), ind(a("ftab"), a("nbu", 304, 384)))
-    tc(a("fl", 3 * V, 4 * V), ind(a("ftab"), a("nbu", 384, 512)))
-    for d in range(D):
-        fold16(a("k2", 128 * d, 128 * d + 128), "hb", lambda c: a("fl", V * d + c, V * d + V, 16))
-    act(a("y2b"), ind(a("xw"), a("l2bu")))
-    act(a("k4", 0, NG), a("y2b"))
-    act(a("k5", 0, NG), a("z1b"))
-    decode("land2", "d2", "lu2", "se2", "ptab2")
-    tt(a("key"), a("code"), a("k2"), Op.mult)
-    tt(a("h2"), a("key", 0, 256), a("key", 256, 512), Op.max)
-    tt(a("q2"), a("h2", 0, 128), a("h2", 128, 256), Op.max)
-    ts(a("l2i"), a("q2"), 4095, Op.bitwise_and)
-    tc(a("l2u"), a("l2i"))
-    act(a("ptab2", SH, SH + 1024), ind(a("gid"), a("l2u", 0, 64)))
-    tc(a("ptab2", SH + 1024, G0), ind(a("gid"), a("l2u", 64, 128)))
-    tt(a("m2b"), ind(a("ptab2"), a("l2bu")), a("gidb"), Op.is_equal)
-    tt(a("t2b"), a("m2b"), a("k4", 0, NG), Op.mult)
-    tt(a("xmb"), a("t2b"), a("k5", 0, NG), Op.add)
-    send(4, "xmb", C, "xm")
-    act(a("pp2", 0, 1024), ind(a("ptab2"), a("l2u", 0, 64)))
-    tc(a("pp2", 1024, 2048), ind(a("ptab2"), a("l2u", 64, 128)))
-    for d in (2, 3):
-        act(a("wb", NG * d, NG * d + NG), ind(a("wa", V * d, V * d + V), a("blu")))
+    tt(a("l2b"), a("l2bi"), a("k1", 96, 120), Op.mult)
+    left3 = send(3, "l2b", 3, "land2")
     for c in range(16):
-        act(a("rm", 128 * c, 128 * c + 128), a("gb"), scale=a("mc", c, c + 1))
-    fold16(a("k3", 0, 128), "hb", lambda c: a("ftab", SH + c, G0, 16))
-    fold16(a("k0", 0, 128), "hh", lambda c: a("pp2", c, 2048, 16))
-    ts(a("vB"), a("v16"), a("cf"), Op.add)
-    ts(a("m1B"), a("k3", 0, 128), -1.0, Op.mult, 1.0, Op.add)
-    tc(a("l1f"), a("l1i"))
-    tc(a("l2f"), a("l2i"))
+        dma("y", a("wa", p0=c, ps=16), lambda: T.w[:, 0:2 * V], after=[left3])
+    ts(a("m1bl"), a("k1", 96, 120), -1.0, Op.mult, 1.0, Op.add)
+    tc(a("l2bu"), a("l2b"))
+    tc(a("se2", 0, 3), slot("l2b", r, 3))
+    tt(a("l1mb"), a("m1bl"), a("l1b"), Op.mult)
+    flags("s", 1, 0)
+    flagfold(1, 0)
+    tt(a("candu"), a("l1mb"), a("l2b"), Op.add)
+    flags("s", 0, 1)
+    flagfold(0, 1)
+
+    def pointers(h):
+        k, c = "k%d" % (2 + h), 64 * h
+        for d in range(3):
+            tt(a("key", 192 * h + 64 * d, 192 * h + 64 * d + 64), a("cs", 128 * d + c, 128 * d + c + 64), a(k, 64 * d, 64 * d + 64), Op.mult)
+        tt(a("h2", 2 * c, 2 * c + 64), a("key", 192 * h, 192 * h + 64), a("key", 192 * h + 64, 192 * h + 128), Op.max)
+        tt(a("h2", 2 * c + 64, 2 * c + 128), a("key", 192 * h + 128, 192 * h + 192), a("cs", 384 + c, 448 + c), Op.max)
+        tt(a("q2", c, c + 64), a("h2", 2 * c, 2 * c + 64), a("h2", 2 * c + 64, 2 * c + 128), Op.max)
+        ts(a("l2i", c, c + 64), a("q2", c, c + 64), 4095, Op.bitwise_and)
+        tt(a("l2u", c, c + 64), a("l2i", c, c + 64), a("k0", c, c + 64), Op.mult)
+
+    flags("v", 2, 1)
+    flagfold(2, 1)
+    pointers(0)
+    flags("s", 1, 1, 0, 40)
+    flags("v", 1, 1, 40, 64)
+    flagfold(1, 1)
+    gather("s", a("od", 50 * r + 1, 50 * r + 49), a("gid"), a("se2", 0, 3))
+    gather("s", a("yc"), a("xw"), a("candu"))
+    gather("v", a("ptab2", SH, SH + 384), a("gid"), a("l2u", 0, 24))
+    gather("s", a("ptab2", SH + 384, SH + 1024), a("gid"), a("l2u", 24, 64))
+    pointers(1)
+    decode("s", "land2", "d2", "lu2", "ptab2")
+    gather("v", a("ptab2", SH + 1024, SH + 1664), a("gid"), a("l2u", 64, 104))
+    gather("s", a("ptab2", SH + 1664, G0), a("gid"), a("l2u", 104, 128))
+    act(a("k4", 0, NG), a("yc"))
+    act(a("m1B"), a("k0", 0, 128), scale=-1.0, bias=1.0)
+    tt(a("m2b"), ind(a("ptab2"), a("l2bu")), a("gq"), Op.is_equal)
+    tt(a("xmb"), a("m2b"), a("k4", 0, NG), Op.mult)
+    send(4, "xmb", C, "xm")
+    gather("s", a("pp2", 0, 1024), a("ptab2"), a("l2u", 0, 64))
+    fold16(a("k6", 0, 64), "hh", "pp2", 0, 1024)
+    gather("v", a("pp2", 1024, 1536), a("ptab2"), a("l2u", 64, 96))
+    gather("s", a("pp2", 1536, 2048), a("ptab2"), a("l2u", 96, 128))
+    fold16(a("k7", 0, 64), "hh", "pp2", 1024, 2048)
     tt(a("l1m"), a("m1B"), a("l1f"), Op.mult)
-    tt(a("m2B"), a("k0", 0, 128), a("vB"), Op.is_equal)
-    tt(a("m2l"), a("m2B"), a("l2f"), Op.mult)
-    tt(a("mu"), a("m2l"), a("l1m"), Op.max)
-    tt(a("xt", SH, G0), ind(a("xw"), a("mu")), a("xo"), Op.add)
+
+    def mates(h):
+        c = 64 * h
+        tt(a("m2B", c, c + 64), a("k%d" % (6 + h), 0, 64), a("vB", c, c + 64), Op.is_equal)
+        tt(a("m2l", c, c + 64), a("m2B", c, c + 64), a("l2i", c, c + 64), Op.mult)
+        tt(a("mu", c, c + 64), a("m2l", c, c + 64), a("l1m", c, c + 64), Op.max)
+
+    def features(h):
+        c = 1024 * h
+        tt(a("xt", SH + c, SH + c + 1024), ind(a("xw"), a("mu", 64 * h, 64 * h + 64)), a("xo", c, c + 1024), Op.add)
+
+    def mates_names(k0, k1):
+        gather("s", a("mg", 16 * k0, 16 * k1), a("gid"), a("mu", k0, k1))
+
+    mates(0)
     act(slot("xm", r, C), slot("xmb", r, C))
-    act(a("mg"), ind(a("gid"), a("mu")))
-    for d in (2, 3):
-        mm(a("k%d" % (4 + d), 0, NG), a("idb"), a("wb", NG * d, NG * d + NG))
+    features(0)
+    mates_names(0, 64)
+    fold16(a("k2", 0, 64), "hh", "mg", 0, 1024)
+    mates(1)
+    for d in range(D):
+        mm(a("k%d" % (4 + d), 0, NG), a("sel", 128 * d, 128 * d + 128), a("wb"))
     mm(a("k1", 0, NG), a("idb"), a("xw", G0, TB), True, False)
     mm(a("k1", 0, NG), a("idb"), a("xm"), False, True)
+    features(1)
+    mates_names(64, 96)
     act(a("xt", G0, TB), a("k1", 0, NG))
-    wcast("k4", 2, 0)
-    wcast("k5", 3, 0)
-    fold16(a("k3", 0, 128), "hh", lambda c: a("mg", c, 2048, 16))
-    ms(a("xt", 0, SH), 0.0)
-    ms(a("st", 0, SH), 0.0)
-    act(a("cmk", 0, 768), ind(a("xt"), a("nbbu", 48, 96)))
-    tt(a("cmk", 768, 1536), ind(a("xt"), a("nbbu", 0, 48)), a("wb", 0, 768), Op.mult)
-    tt(a("k6", 0, NG), a("cmk", 0, NG), a("k6", 0, NG), Op.mult)
-    tt(a("qb"), a("cmk", NG, 768), a("k7", 0, NG), Op.mult)
-    tt(a("k6", 0, NG), a("cmk", 768, 768 + NG), a("k6", 0, NG), Op.add)
-    tt(a("k6", 0, NG), a("qb"), a("k6", 0, NG), Op.add)
-    tt(a("sb"), a("cmk", 768 + NG, 1536), a("k6", 0, NG), Op.add)
-    send(5, "sb", C, "st", G0)
-    wcast("k6", 2, 512)
-    wcast("k7", 3, 512)
+    mates_names(96, 128)
+    fold16(a("k2", 64, 128), "hh", "mg", 1024, 2048)
+
+    def near(i):
+        k0, k1, t = PIECES[i]
+        for d in (0, 1):
+            tt(a("pr", V * d + 16 * k0, V * d + 16 * k1), ind(a("xt"), a("nbu", 128 * d + k0, 128 * d + k1)),
+               a("wa", V * d + 16 * k0, V * d + 16 * k1), Op.mult)
+
+    def wcast(i):
+        k0, k1, t = PIECES[i]
+        for d in (2, 3):
+            mm(a("k%d" % (2 + d + 2 * (i % 2)), 0, 16 * (k1 - k0)), a("sel", 128 * d, 128 * d + 128), a("w16", 16 * k0, 16 * k1))
 
     def gather23(i):
-        for d, b in ((2, "g2"), (3, "g3")):
-            act(a(b, 512 * i, 512 * i + 512), ind(a("xt"), a("nbu", 128 * d + 32 * i, 128 * d + 32 * i + 32)))
+        k0, k1, t = PIECES[i]
+        for d in (2, 3):
+            gather("s", a("pr", V * d + 16 * k0, V * d + 16 * k1), a("xt"), a("nbu", 128 * d + k0, 128 * d + k1))
 
-    def products(i, w2, w3, keep):
-        u, ub = 1024 * (i % 2), "ptab2" if i < 2 else "uu"
-        for d in (0, 1):
-            tt(a(ub, u + 512 * d, u + 512 * d + 512), ind(a("xt"), a("nbu", 128 * d + 32 * i, 128 * d + 32 * i + 32)),
-               a("wa", V * d + 512 * i, V * d + 512 * i + 512), Op.mult)
-        x2, x3 = a("g2", 512 * i, 512 * i + 512), a("g3", 512 * i, 512 * i + 512)
-        tt(a(w2) if keep else x2, x2, a(w2), Op.mult)
-        tt(x3, x3, a(w3), Op.mult)
+    def far(i):
+        k0, k1, t = PIECES[i]
+        n = 16 * (k1 - k0)
+        p = [a("pr", V * d + 16 * k0, V * d + 16 * k1) for d in range(D)]
+        w2, w3 = [a("k%d" % (2 + d + 2 * (i % 2)), 0, n) for d in (2, 3)]
+        out = a("st", SH + 16 * k0, SH + 16 * k1)
+        if t == 0:
+            tt(w2, p[2], w2, Op.mult)
+            tt(p[3], p[3], w3, Op.mult)
+            tt(w2, p[0], w2, Op.add)
+            tt(w2, p[1], w2, Op.add)
+            return lambda: tt(out, p[3], w2, Op.add)
+        k = a("k%d" % (i % 2), 0, n)
+        tt(p[2], p[2], w2, Op.mult)
+        tt(p[3], p[3], w3, Op.mult)
+        for d in range(t):
+            mm(k, a("idf"), p[d], d == 0, d == t - 1)
+        if t == 3:
+            return lambda: tt(out, p[3], k, Op.add)
+        return lambda: act(out, k)
 
-    def sum_v(i, w2):
-        u, ub = 1024 * (i % 2), "ptab2" if i < 2 else "uu"
-        tt(a(w2), a(ub, u, u + 512), a(w2), Op.add)
-        tt(a(w2), a("g3", 512 * i, 512 * i + 512), a(w2), Op.add)
-        tt(a("st", SH + 512 * i, SH + 512 * i + 512), a(ub, u + 512, u + 1024), a(w2), Op.add)
-
-    def sum_t(i, k):
-        u, ub = 1024 * (i % 2), "ptab2" if i < 2 else "uu"
-        xs = (a(ub, u, u + 512), a(ub, u + 512, u + 1024), a("g2", 512 * i, 512 * i + 512), a("g3", 512 * i, 512 * i + 512))
-        for j, x in enumerate(xs):
-            mm(a(k), a("idf"), x, j == 0, j == 3)
-
-    gather23(0)
-    tt(a("rep"), a("k3", 0, 128), a("vB"), Op.is_gt)
-    mm(a("k1", 0, 128), a("gb"), a("rep"))
-    mm(a("k2", 0, 128), a("tri"), a("rep"))
-    op("v", lambda: g.vector.tensor_tensor_scan(ap(a("sc")), ap(a("k1", 0, 128)), ap(a("zz")), 0.0, Op.add, Op.add),
-       [a("sc")], [a("k1", 0, 128), a("zz")])
-    tt(a("nin"), a("sc"), a("k2", 0, 128), Op.add)
-    ts(a("na"), a("nin"), float(BK), Op.add)
-    tt(a("nm"), a("na"), a("rep"), Op.mult)
-    ts(a("numh"), a("nm"), -float(BK + 1), Op.add)
-    products(0, "k4", "k5", False)
-    for b in range(4):
+    near(0)
+    for d in range(D):
+        gather("s", a("cmk", NG * d, NG * d + NG), a("xt"), a("nbbu", 24 * d, 24 * d + 24))
+    tt(a("rep"), a("k2", 0, 128), a("vB"), Op.is_gt)
+    mm(a("k2", 0, 128), a("gb"), a("rep"))
+    mm(a("k3", 0, 128), a("tri"), a("rep"))
+    b = [a("cmk", NG * d, NG * d + NG) for d in range(D)]
+    w = [a("k%d" % (4 + d), 0, NG) for d in range(D)]
+    tt(w[0], b[0], w[0], Op.mult)
+    tt(b[1], b[1], w[1], Op.mult)
+    op("v", lambda: g.vector.tensor_tensor_scan(ap(a("sc")), ap(a("k2", 0, 128)), ap(a("zz")), 0.0, Op.add, Op.add),
+       [a("sc")], [a("k2", 0, 128), a("zz")])
+    tt(w[0], b[1], w[0], Op.add)
+    tt(a("nin"), a("sc"), a("k3", 0, 128), Op.add)
+    for bk in range(4):
         for c in range(16):
-            mm(a("k%d" % b, c, 512, 16), a("rm", 128 * c, 128 * c + 128), a("numh", 32 * b, 32 * b + 32))
-    wcast("k4", 2, 1024)
-    wcast("k5", 3, 1024)
-    gather23(1)
-    for b in range(4):
-        act(a("numt", SH + 512 * b, SH + 512 * b + 512), a("k%d" % b), bias=float(V * r))
-    ms(a("numt", 0, SH), -65536.0)
-    sum_t(0, "k0")
-    act(a("numb"), ind(a("numt", SH, G0), a("blu")))
-    act(slot("st", r, C, G0), slot("sb", r, C))
-    act(slot("numt", r, C, G0), slot("numb", r, C))
+            mm(a("k%d" % bk, c, 512, 16), a("zsl", 16 + c, 144 + c), a("nin", 32 * bk, 32 * bk + 32))
+    tt(b[2], b[2], w[2], Op.mult)
+    tt(w[0], b[2], w[0], Op.add)
+    tt(b[3], b[3], w[3], Op.mult)
+    tt(a("sb"), b[3], w[0], Op.add)
+    send(5, "sb", C, "st", G0)
+    wcast(0)
+    gather23(0)
+    wcast(1)
+    near(1)
+    for bk in range(4):
+        act(a("numt", SH + 512 * bk, SH + 512 * bk + 512), a("k%d" % bk), scale=a("sc1"), bias=a("bi1"))
+        if bk == 1:
+            act(slot("st", r, C, G0), slot("sb", r, C))
+            act(a("na"), a("nin"), bias=float(V - 1))
+            gather23(1)
+    end0 = far(0)
+    gather("s", a("numb"), a("numt", SH, G0), a("blu"))
     send(6, "numb", C, "numt", G0)
-    products(1, "k6", "k7", False)
+    wcast(2)
+    end1 = far(1)
     gather23(2)
-    sum_t(1, "k1")
-    wcast("k6", 2, 1536)
-    wcast("k7", 3, 1536)
-    gather23(3)
-    act(a("st", SH, SH + 512), a("k0"))
-    act(a("st", SH + 512, SH + 1024), a("k1"))
-    products(2, "k4", "k5", True)
-    sum_v(2, "k4")
-    ts(a("po"), a("nm"), float(V - 1 - BK), Op.add)
-    ts(a("numf"), a("nm"), float(V * r - BK - 1), Op.add)
-    tt(a("posu"), a("po"), a("vB"), Op.max)
-    products(3, "k6", "k7", True)
-    sum_v(3, "k6")
-    act(a("ptab1", 0, V), ind(a("numt"), a("mu")))
-    fold16(a("k2", 0, 128), "hf", lambda c: a("ptab1", c, V, 16))
-    cuts = (128, 96, 48, 16, 0)
-    for k1, k0 in zip(cuts, cuts[1:]):
-        act(a("g2", 16 * k0, 16 * k1), ind(a("st"), a("mu", k0, k1)))
+    act(a("numf"), a("nin"), bias=float(V * r - 1))
+    act(slot("numt", r, C, G0), slot("numb", r, C))
+    tt(a("nm"), a("na"), a("rep"), Op.mult)
+    for k0, k1, t in PIECES:
+        ts(a("mur", k0, k1), a("mu", k0, k1), -float(8 + 16 * k0), Op.add, 0.0, Op.max)
+    tt(a("posu"), a("nm"), a("vB"), Op.max)
     last = []
-    for i, (k1, k0) in enumerate(zip(cuts, cuts[1:])):
-        if i == 3:
-            tt(a("cmo"), a("k2", 0, 128), a("numf"), Op.max)
-            last.append(dma("y", lambda: T.cm[:, :], a("cmo")))
-        tt(ind(a("yw", 0, V + 16 * k1), a("posu", k0, k1)), a("st", SH + 16 * k0, SH + 16 * k1), a("g2", 16 * k0, 16 * k1), Op.add)
-        last.append(dma("y", (lambda c0, c1: lambda: T.y[:, c0:c1])(16 * k0, 16 * k1), a("yw", V + 16 * k0, V + 16 * k1)))
+
+    def mates_sums(i):
+        k0 = PIECES[i][0]
+        for c1, c0 in zip(CUTS[i], CUTS[i][1:]):
+            gather("s", a("g2", 16 * c0, 16 * c1), a("st", 8 + 16 * k0, TB), a("mur", c0, c1))
+
+    def scatter(i):
+        for c1, c0 in zip(CUTS[i], CUTS[i][1:]):
+            tt(ind(a("yw", 0, V + 16 * c1), a("posu", c0, c1)), a("st", SH + 16 * c0, SH + 16 * c1), a("g2", 16 * c0, 16 * c1), Op.add)
+            last.append(dma("y", (lambda c0, c1: lambda: T.y[:, c0:c1])(16 * c0, 16 * c1), a("yw", V + 16 * c0, V + 16 * c1)))
+
+    def mates_numbers(h):
+        gather("s", a("nmate", 1024 * h, 1024 * h + 1024), a("numt"), a("mu", 64 * h, 64 * h + 64))
+        fold16(a("k2", 64 * h, 64 * h + 64), "hh2", "nmate", 1024 * h, 1024 * h + 1024)
+
+    near(2)
+    end0()
+    wcast(3)
+    gather23(3)
+    end2 = far(2)
+    mates_sums(0)
+    ts(a("pZ"), a("cf"), 1.0, Op.is_gt, 1000.0, Op.mult)
+    near(3)
+    end1()
+    tt(a("pY"), a("pZ"), a("p16"), Op.add)
+    mates_sums(1)
+    end3 = far(3)
+    ts(a("hh2"), a("jj", 0, 144), a("pY"), Op.is_equal, a("pS"), Op.mult)
+    mates_numbers(0)
+    scatter(0)
+    end2()
+    mates_sums(2)
+    scatter(1)
+    end3()
+    mates_numbers(1)
+    mates_sums(3)
+    scatter(2)
+    tt(a("cmo"), a("k2", 0, 128), a("numf"), Op.min)
+    last.append(dma("y", lambda: T.cm[:, :], a("cmo")))
+    scatter(3)
     ops.append({"q": "y", "fn": None, "dep": set(last), "inc": 0, "sem": None, "waits": [], "K": 0})
 
     known = {q: 0 for q in "vstgy"}
@@ -535,4 +623,5 @@ def rank_program(g, core, T, topo):
             x = o["fn"]()
             if i in where:
                 x.then_inc(T.sem[where[i]], o["inc"])
-    g.wait_ge(T.sem["sent"], sent[0])
+    for k in range(7):
+        g.wait_ge(T.sem["t%d" % k], engines)

@@ -6,33 +6,39 @@ NG = N * C
 SH = 16
 G0 = SH + V
 TB = G0 + NG
+TOP = 3 * 4096 + 1024
 BIG = 4096
-PIECES = ((96, 128, 3), (64, 96, 3), (32, 64, 3), (0, 32, 3))
+PIECES = ((96, 128, 4), (64, 96, 3), (32, 64, 3), (0, 32, 3))
+NEARS = ((2, 2, 2, 2), (2, 2, 2, 2))
+JOIN = (0, 0, 0, 0)
+BANKS = (("k1", "k0", "k2", "k3"), ("k0", "k7", "k2", "k3"), ("k1", "k4", "k5", "k6"), ("k5", "k7", "k2", "k3"))
+XS = 768
 CUTS = ((128, 96), (96, 64), (64, 32), (32, 12, 0))
 
 _F, _B, _I, _H, _U = "float32", "bfloat16", "int32", "float16", "uint16"
 _LOG = {n: (w, t) for n, w, t in [
-    ("pf", 1, _F), ("pi", 1, _I), ("ci", 1, _I), ("cf", 1, _F), ("c1000", 1, _F), ("p16", 1, _F), ("pX", 1, _F), ("pY", 1, _F),
-    ("pZ", 1, _F), ("pS", 1, _F), ("sc1", 1, _F), ("bi1", 1, _F), ("u32", 32, _F), ("ee", 32, _B), ("dm", 48, _B),
-    ("jj", 160, _F), ("jm", 128, _F), ("v16", 128, _F), ("vB", 128, _F), ("basec", 24, _F), ("selfc", 3, _F), ("cols", 16, _F),
+    ("pf", 1, _F), ("pi", 1, _I), ("ci", 1, _I), ("cf", 1, _F), ("c1000", 1, _F), ("p16", 1, _F), ("pX", 1, _F),
+    ("pY", 1, _F), ("pZ", 1, _F), ("pS", 1, _F), ("hh2", 144, _H), ("ninT", 128, _F),
+    ("u32", 32, _F), ("ee", 32, _B), ("dm", 48, _B),
+    ("jj", 160, _F), ("jm", 128, _F), ("v16", 128, _F), ("vB", 128, _F), ("rel1", 24, _F), ("rel2", 24, _F), ("selfc", 3, _U),
     ("mc", 16, _F), ("idb", 128, _B), ("idf", 128, _F), ("ip", 128, _B), ("inn", 128, _B), ("zsl", 160, _H), ("gsh", 144, _H),
-    ("gsf", 144, _F), ("hb", 144, _B), ("hh", 144, _H), ("hh2", 144, _H), ("gb", 128, _B), ("tri0", 128, _B), ("tri", 128, _B),
+    ("gsf", 144, _F), ("hb", 144, _B), ("hh", 144, _H), ("hf", 144, _F), ("gb", 128, _B), ("tri0", 128, _B), ("tri", 128, _B),
     ("sel", 512, _B), ("zz", 128, _F), ("gid", TB, _F), ("od", 400, _F),
     ("wr", V, _B), ("w16", V, _B), ("nbi", 512, _I), ("bli", 24, _I), ("xw", TB, _B), ("xo", V, _B), ("wa", 2 * V, _B),
-    ("nbu", 512, _U), ("nbc", 512, _F), ("blu", 24, _U), ("blh", 24, _I), ("blx", 24, _U), ("bll", 24, _I), ("blo", 24, _U),
+    ("nbu", 512, _U), ("ones", 128, _H), ("base", 512, _H), ("blu", 24, _U), ("blh", 24, _I), ("blx", 24, _U), ("bll", 24, _I), ("blo", 24, _U),
     ("gidb", NG, _F), ("mask", NG, _F), ("xb", NG, _B),
-    ("gt", 768, _B), ("code", 512, _F), ("cs", 512, _I), ("lo", 256, _I), ("q1", 128, _F), ("l1u", 128, _U), ("n3i", 384, _I),
-    ("n3u", 384, _U), ("l1s", 128, _F), ("l1f", 128, _F), ("lm", NG, _H), ("l1b", 24, _F), ("l1bu", 24, _U), ("land1", 24, _F),
-    ("d1", 24, _F), ("lu1", 24, _U), ("se1", 4, _U), ("ptab1", TB, _F), ("ftab", TB, _B), ("m1B", 128, _F), ("l1m", 128, _F),
-    ("cmk", 1536, _F), ("codeb", 96, _I), ("nbba", 96, _I), ("nbbu", 96, _U), ("wb", NG, _B), ("gq", NG, _F),
-    ("fb", 5 * NG, _B), ("kb", 96, _F), ("h2b", 48, _F), ("q2b", 24, _I), ("l2bi", 24, _I), ("l2b", 24, _F), ("l2bu", 24, _U),
-    ("m1bl", 24, _F), ("l1mb", 24, _F), ("candu", 24, _U), ("yc", NG, _B),
-    ("fl", 3 * V, _B), ("key", 384, _F), ("h2", 256, _F), ("q2", 128, _I), ("l2i", 128, _I), ("l2u", 128, _U),
-    ("land2", 24, _F), ("d2", 24, _F), ("lu2", 24, _U), ("se2", 4, _U), ("ptab2", TB, _F),
-    ("m2b", NG, _B), ("xmb", NG, _B), ("xm", NG, _B),
-    ("pp2", V, _H), ("m2B", 128, _F), ("m2l", 128, _F), ("mu", 128, _U), ("mur", 128, _U),
-    ("mg", V, _H), ("rep", 128, _B), ("sc", 128, _F), ("nin", 128, _H), ("na", 128, _F), ("nm", 128, _F),
-    ("numf", 128, _F), ("posu", 128, _U), ("numt", TB, _F), ("numb", NG, _F), ("nmate", V, _H), ("cmo", 128, _F),
+    ("gt", 768, _B), ("code", 512, _F), ("cs", 512, _I), ("hi", 512, _F), ("lo", 256, _F), ("q1", 128, _F), ("l1u", 128, _U), ("n3i", 384, _I),
+    ("n3u", 384, _U), ("l1s", 128, _F), ("l1f", 128, _F), ("lm", NG, _H), ("l1b", 24, _F), ("l1bu", 24, _U), ("csh", 384, _F),
+    ("d1", 24, _F), ("out1", 24, _U), ("lu1", 24, _U), ("se1", 4, _U), ("ptab1", TB, _F), ("ftab", TB, _B),
+    ("f1b", NG, _B), ("m1B", 128, _F), ("keep", 128, _F), ("q1b", 24, _F), ("m1bl", 24, _F), ("keepb", 24, _F),
+    ("cmk", 1536, _F), ("codeb", 96, _I), ("nbba", 96, _I), ("nbbu", 96, _U), ("wb", NG, _B),
+    ("fb", 4 * NG, _B), ("kb", 96, _F), ("h2b", 48, _F), ("h3b", 24, _F), ("q2b", 24, _I), ("l2bi", 24, _I), ("l2bu", 24, _U),
+    ("yc", NG, _B), ("fl", 3 * V, _B), ("key", 512, _F), ("h2", 256, _F), ("q2", 128, _I), ("l2i", 128, _I), ("l2u", 128, _U),
+    ("out2", 24, _U), ("d2", 24, _F), ("lu2", 24, _U), ("se2", 4, _U), ("ptab2", TB, _F),
+    ("m2b", NG, _B), ("xmb", NG, _B), ("xm", NG, _B), ("xg", XS, _B),
+    ("pp2", V, _H), ("m2B", 128, _F), ("mu", 128, _U), ("mur", 128, _U),
+    ("gtc", 128, _B), ("vT", 128, _F), ("rep", 128, _B), ("sc", 128, _F), ("nin", 128, _H), ("na", 128, _F), ("nm", 128, _F),
+    ("numf", 128, _F), ("posu", 128, _U), ("numt", TB, _F), ("numb", NG, _H), ("numg", NG, _H), ("nmate", V, _H), ("cmo", 128, _F),
     ("xt", TB, _F), ("sb", NG, _F), ("st", TB, _F), ("pr", 4 * V, _F), ("g2", V, _F), ("yw", 2 * V, _F),
 ]}
 _WHERE, SCRATCH, _fill = {}, {}, {}
@@ -51,7 +57,7 @@ for _n, _w in _PSUM.items():
     _WHERE[_n] = (_n, 0)
     _LOG[_n] = (_w, _F)
 NPOOL = 130
-SEMAPHORES = ["e%d" % k for k in range(7)] + ["t%d" % k for k in range(7)] + ["s%d" % i for i in range(NPOOL)]
+SEMAPHORES = ["e%d" % k for k in range(8)] + ["t%d" % k for k in range(8)] + ["s%d" % i for i in range(NPOOL)]
 
 
 def a(name, c0=0, c1=None, cs=1, p0=0, p1=128, ps=1):
@@ -74,17 +80,22 @@ def _clash(s, t):
     return True
 
 
-def _plan(src, topo, cores):
+def _plan(src, topo, dsts):
     used, out = set(), {}
     for far in (True, False):
-        for dst in cores:
-            if dst == src or (topo.chip(dst) != topo.chip(src)) != far:
-                continue
+        todo = [dst for dst in dsts if (topo.chip(dst) != topo.chip(src)) == far]
+        for i, dst in enumerate(todo):
             free = [x for x in topo.engines(src, dst) if x not in used]
-            e = free[:2] if far else free[-2:]
-            used.update(e)
-            out[dst] = e
+            n = 1 << ((len(free) // (len(todo) - i)).bit_length() - 1)
+            used.update(free[:n])
+            out[dst] = free[:n]
     return out
+
+
+def _targets(k, q, chips):
+    if k in (0, 7):
+        return [p for p in range(N) if p != q and (chips[p] == chips[q]) == (k == 0)]
+    return range(q) if k == 5 else range(q + 1, N) if k == 6 else [p for p in range(N) if p != q]
 
 
 def rank_program(g, core, T, topo):
@@ -93,6 +104,7 @@ def rank_program(g, core, T, topo):
         return
     ops, acc = [], {}
     mmgroup = {}
+    NEAR = NEARS[r * len(NEARS) // N]
     eng = {"v": g.vector, "s": g.scalar, "t": g.tensor, "g": g, "y": g.sync}
 
     def ap(s):
@@ -156,18 +168,18 @@ def rank_program(g, core, T, topo):
     def ms(out, c):
         op("v", lambda: g.vector.memset(ap(out), c), [out], [])
 
-    def act(out, x, scale=1.0, bias=None):
+    def act(out, x, scale=1.0, bias=None, func=Fn.Identity):
         if bias is None:
             op("s", lambda: g.scalar.activation(out=ap(out), in_=ap(x), func=Fn.Copy, scale=ap(scale)), [out], [x, scale])
         else:
-            op("s", lambda: g.scalar.activation(out=ap(out), in_=ap(x), func=Fn.Identity, bias=ap(bias), scale=ap(scale)),
+            op("s", lambda: g.scalar.activation(out=ap(out), in_=ap(x), func=func, bias=ap(bias), scale=ap(scale)),
                [out], [x, scale, bias])
 
     def gather(q, out, win, off):
         (tc if q == "v" else act)(out, ind(win, off))
 
-    def mm(out, l, rr, start=True, stop=True):
-        op("t", lambda: g.tensor.matmul(ap(out), ap(l), ap(rr), start, stop), [out], [l, rr], stop=stop)
+    def mm(out, l, rr, start=True, stop=True, signal=False):
+        op("t", lambda: g.tensor.matmul(ap(out), ap(l), ap(rr), start, stop), [out], [l, rr], stop=stop or signal)
 
     def iota(out, pattern, base, cm):
         if _LOG[out[0]][1] != _I:
@@ -180,9 +192,11 @@ def rank_program(g, core, T, topo):
         return op(q, lambda: eng[q].dma_start(out=f(out), in_=f(x)), [out] if isinstance(out, tuple) else [], regs([x]), inc=16,
                   after=after)
 
-    plan = _plan(core, topo, T.cores)
-    expect = sum(len(_plan(c, topo, T.cores)[core]) for c in T.cores if c != core)
-    engines = sum(len(e) for e in plan.values())
+    def _to(k, q):
+        return _targets(k, q, [topo.chip(c) for c in T.cores])
+
+    plans = [[_plan(T.cores[q], topo, [T.cores[p] for p in _to(k, q)]) for q in range(N)] for k in range(8)]
+    engines = [sum(len(e) for e in plans[k][r].values()) for k in range(8)]
 
     def slot(name, q, w, base=0):
         return a(name, base + w * q, base + w * q + w)
@@ -193,32 +207,33 @@ def rank_program(g, core, T, topo):
 
     def arrive(k, name, w, base=0):
         for q in range(N):
-            if q != r:
+            if r in _to(k, q):
                 acc.setdefault(name, []).append((len(ops), True, slot(name, q, w, base)))
-        event("e%d" % k, expect)
+        event("e%d" % k, sum(len(plans[k][q].get(core, ())) for q in range(N)))
 
     def send(k, name, w, dname, base=0, sbase=0):
         dst = slot(dname, r, w, base)
 
         def fn():
             tr = []
-            for q in range(N):
-                if q != r:
-                    rid, pid, _se = topo.addr(T.cores[q])
-                    tr.append(RemoteDMATransfer(dst_ids=[DstId(rid=rid, pnc=pid)], dma_engine_mask=sum(1 << e for e in plan[T.cores[q]]),
-                                                remote_sem=T.sem["e%d" % k], src=ap(slot(name, q, w, sbase)), dst=ap(dst)))
+            for q in _to(k, r):
+                rid, pid, _se = topo.addr(T.cores[q])
+                tr.append(RemoteDMATransfer(dst_ids=[DstId(rid=rid, pnc=pid)], dma_engine_mask=sum(1 << e for e in plans[k][r][T.cores[q]]),
+                                            remote_sem=T.sem["e%d" % k], src=ap(slot(name, q, w, sbase)), dst=ap(dst)))
             g.remote_dma_fused(tr, local_sem=T.sem["t%d" % k])
-        op("g", fn, [], [slot(name, q, w, sbase) for q in range(N) if q != r])
-        return event("t%d" % k, engines)
+        if engines[k]:
+            op("g", fn, [], [slot(name, q, w, sbase) for q in _to(k, r)])
+        return event("t%d" % k, engines[k])
 
     def fold16(out, lhs, name, c0, c1):
         for c in range(16):
             mm(out, a(lhs, 16 - c, 144 - c), a(name, c0 + c, c1, 16), c == 0, c == 15)
 
-    for k, name, w, base in ((0, "xw", C, G0), (1, "land1", 3, 0), (2, "ftab", C, G0), (3, "land2", 3, 0), (4, "xm", C, 0),
-                             (5, "st", C, G0), (6, "numt", C, G0)):
+    for k, name, w, base in ((0, "xw", C, G0), (1, "lu1", 3, 0), (2, "ftab", C, G0), (3, "lu2", 3, 0), (4, "xm", C, 0),
+                             (5, "st", C, G0), (6, "numg", C, 0), (7, "xw", C, G0)):
         arrive(k, name, w, base)
     me = G0 + C * r
+    low, high = C * (r + 1), C * (r - r % 2)
 
     dma("y", a("wr", p1=32), lambda: T.w[:, :])
     dma("s", a("bli"), lambda: T.bl[:, :])
@@ -231,7 +246,8 @@ def rank_program(g, core, T, topo):
     iota(a("jm"), [[16, 8], [0, 16]], 0, 0)
     iota(a("gid", SH, SH + 512), [[1, 512]], 0, 0)
     iota(a("v16"), [[16, 128]], 0, 0)
-    iota(a("basec"), [[50, 8], [0, 3]], 1 - me, 0)
+    iota(a("rel1"), [[-C, 8], [0, 3]], 50 * r + 1 - G0 + 1024, 0)
+    iota(a("rel2"), [[-C, 8], [0, 3]], 50 * r + 1 - G0, 0)
     ms(a("od"), float(BIG))
     ts(a("ee"), a("u32"), 0.0, Op.is_equal)
     tt(a("dm", 0, 24), a("ee", 8, 32), a("ee", 0, 24), Op.subtract)
@@ -247,23 +263,20 @@ def rank_program(g, core, T, topo):
     ts(a("zsl"), a("jj"), a("pf"), Op.is_equal)
     ts(a("mc"), a("jj", 16, 32), a("cf"), Op.is_equal)
     tt(a("p16"), a("pf"), a("cf"), Op.subtract)
-    ts(a("c1000"), a("cf"), 1000.0, Op.mult)
     act(a("ip"), a("zsl", 16, 144), scale=4096.0)
     act(a("inn"), a("zsl", 16, 144), scale=-4096.0)
-    act(a("idb"), a("zsl", 16, 144))
-    act(a("idf"), a("zsl", 16, 144))
+    act(a("ones"), a("zsl", 16, 144), scale=0.0, bias=1.0)
+    for d in range(D):
+        act(a("base", 128 * d, 128 * d + 128), a("zsl", 16, 144), scale=float(SH + (3 - d) * 4096 - TOP))
     ts(a("gsh"), a("jj", 0, 144), a("p16"), Op.is_equal)
-    tt(a("pX"), a("c1000"), a("pf"), Op.add)
-    ts(a("tri0"), a("jj", 16, 144), a("pf"), Op.is_lt, -1.0, Op.mult)
-    ts(a("hb"), a("jj", 0, 144), a("pX"), Op.is_equal)
+    ts(a("pX"), a("cf"), 1000.0, Op.mult, a("pf"), Op.add)
     ts(a("bll"), a("bli"), 15, Op.bitwise_and)
     ts(a("blh"), a("bli"), 4, Op.logical_shift_right)
     tc(a("blu"), a("bli"))
     tc(a("blo"), a("bll"))
     tc(a("blx"), a("blh"))
+    ts(a("hb"), a("jj", 0, 144), a("pX"), Op.is_equal)
     ts(a("gb"), a("jm"), a("p16"), Op.is_equal)
-    for d in range(D):
-        ts(a("sel", 128 * d, 128 * d + 128), a("jm"), float(d), Op.add, a("pf"), Op.is_equal)
     gather("s", a("mask"), a("mc"), a("blo"))
     act(a("gid", SH + 512, SH + 1024), a("gid", SH, SH + 512), bias=512.0)
     for b in (0, 1):
@@ -279,29 +292,35 @@ def rank_program(g, core, T, topo):
     g01, g12, g23, g02, g13, g03 = [a("gt", 128 * i, 128 * i + 128) for i in range(6)]
     for d, terms in enumerate((((g01, -1), (g02, -1), (g03, -1)), ((g01, 1), (g12, -1), (g13, -1)),
                                ((g12, 1), (g23, -1), (g02, 1)), ((g23, 1), (g13, 1), (g03, 1)))):
+        mm(a("k2", 128 * d, 128 * d + 128), a("ones"), a("base", 128 * d, 128 * d + 128), True, False)
         for i, (s, sg) in enumerate(terms):
-            mm(a("k2", 128 * d, 128 * d + 128), s, a("ip" if sg > 0 else "inn"), i == 0, i == 2)
-    ts(a("vB"), a("v16"), a("cf"), Op.add)
-    ts(a("selfc"), a("v16", 0, 3), a("cf"), Op.add, float(me), Op.add)
-    for land in ("land1", "land2"):
+            mm(a("k2", 128 * d, 128 * d + 128), s, a("ip" if sg > 0 else "inn"), False, i == 2)
+    ts(a("selfc"), a("v16", 0, 3), a("cf"), Op.add, float(50 * r + 1), Op.add)
+    for land in ("lu1", "lu2"):
         dma("y", slot(land, r, 3), a("selfc"))
-    tt(a("tri"), a("tri0"), a("gb"), Op.mult)
     for d in range(D):
-        ts(a("nbc", 128 * d, 128 * d + 128), a("nbi", 128 * d, 128 * d + 128), float(SH + (3 - d) * 4096), Op.add)
+        ts(a("sel", 128 * d, 128 * d + 128), a("jm"), float(d), Op.add, a("pf"), Op.is_equal)
+    ts(a("tri0"), a("jj", 16, 144), a("pf"), Op.is_lt, -1.0, Op.mult)
     act(slot("gid", r, C, G0), slot("gidb", r, C))
     act(a("gsf"), a("gsh"))
-    act(a("hh"), a("hb"))
-    tt(a("code"), a("k2"), a("nbc"), Op.add)
-    tt(a("cs", 0, 256), a("code", 0, 256), a("code", 256, 512), Op.max)
-    tt(a("q1"), a("cs", 0, 128), a("cs", 128, 256), Op.max)
-    ts(a("l1s"), a("q1"), -float(3 * 4096 + 1024), Op.add)
-    ts(a("l1u"), a("q1"), -float(3 * 4096), Op.add)
+    tt(a("code", 0, 256), a("k2", 0, 256), a("nbi", 0, 256), Op.add)
+    tt(a("k1", 0, 256), a("k2", 256, 512), a("nbi", 256, 512), Op.add)
+    tt(a("hi", 0, 256), a("code", 0, 256), a("k1", 0, 256), Op.max)
+    tt(a("l1s"), a("hi", 0, 128), a("hi", 128, 256), Op.max)
     tt(a("lm"), ind(a("l1s"), a("blx")), a("mask"), Op.mult)
+    act(a("l1u"), a("l1s"), bias=1024.0)
     fold16(a("k3", 0, 24), "gsh", "lm", 0, NG)
+    tt(a("lo"), a("code", 0, 256), a("k1", 0, 256), Op.min)
+    act(a("code", 256, 512), a("k1", 0, 256))
     gather("s", a("ptab1", SH, G0), a("gid"), a("l1u"))
-    tt(a("lo"), a("code", 0, 256), a("code", 256, 512), Op.min)
+
+    def encode(out, dd, x, rel):
+        tt(a(dd), x, a(rel), Op.add)
+        ts(a(out), a(dd), float(50 * r), Op.max, float(50 * r + C + 1), Op.min)
+
+    encode("out1", "d1", a("k3", 0, 24), "rel1")
+    left1 = send(1, "out1", 3, "lu1")
     ts(a("l1b"), a("k3", 0, 24), 1024.0, Op.add)
-    left1 = send(1, "l1b", 3, "land1")
     iota(a("yw", V, V + 1024), [[0, 1024]], 0, 0)
     for c in range(16):
         dma("y", a("w16", p0=c, ps=16), (lambda d: lambda: T.w[:, V * d:V * d + V])(c % D), after=[left1])
@@ -311,54 +330,67 @@ def rank_program(g, core, T, topo):
     ms(a("ptab1", 0, SH), float(BIG))
     for d in range(D):
         tt(a("cmk", NG * d, NG * d + NG), ind(a("code", 128 * d, 128 * d + 128), a("blx")), a("mask"), Op.mult)
-    for name in ("xw", "ftab", "xt", "st"):
-        ms(a(name, 0, SH), 0.0)
-    ms(a("ptab2", 0, SH), float(BIG))
+    tt(a("hi", 256, 384), a("lo", 0, 128), a("lo", 128, 256), Op.max)
+    tt(a("hi", 384, 512), a("lo", 0, 128), a("lo", 128, 256), Op.min)
+    ts(a("vB"), a("v16"), a("cf"), Op.add)
+    tt(a("tri"), a("tri0"), a("gb"), Op.mult)
     for q in range(N):
         if q != r:
             act(a("od", 50 * q + 1, 50 * q + 49), slot("gidb", q, C))
     gather("s", a("od", 50 * r + 1, 50 * r + 49), a("gid"), a("se1", 0, 3))
+    act(a("cs"), a("hi"), bias=float(TOP))
+    fold16(a("k4", 0, 96), "gsf", "cmk", 0, 1536)
+
+    gather("v", a("ptab1", G0, G0 + 192), a("od"), a("lu1", 0, 12))
+    gather("s", a("ptab1", G0 + 192, TB), a("od"), a("lu1", 12, 24))
+    tt(a("f1b"), ind(a("ptab1"), a("l1bu")), a("gidb"), Op.not_equal)
+    send(2, "f1b", C, "ftab", G0)
+    left2 = send(7, "xb", C, "xw", G0)
+    iota(a("yw", V + 1024, 2 * V), [[0, 1024]], 0, 0)
+    iota(a("vT"), [[0, 8], [1, 16]], 0, 16)
+    dma("y", a("xo"), lambda: T.x[:, :], after=[left2])
+    fold16(a("k5", 0, 24), "hb", "f1b", 0, NG)
+    act(slot("ftab", r, C, G0), slot("f1b", r, C))
+    for h in (0, 1):
+        for d in range(3):
+            act(a("csh", 192 * h + 64 * d, 192 * h + 64 * d + 64), a("cs", 128 * d + 64 * h, 128 * d + 64 * h + 64))
+    act(a("hf"), a("hb"))
+    act(a("hh"), a("hb"))
+    act(a("q1b"), a("l1b"), bias=float(3 * 4096))
+    act(a("q1"), a("l1s"), bias=float(TOP))
     act(slot("xw", r, C, G0), slot("xb", r, C))
-    act(a("l1f"), a("q1"), bias=-float(3 * 4096))
-    for d in range(D):
-        act(a("nbu", 128 * d, 128 * d + 128), a("nbc", 128 * d, 128 * d + 128), bias=-float((3 - d) * 4096))
+    for name in ("xw", "ftab", "xt", "st"):
+        act(a(name, 0, SH), a("jm", 0, SH), scale=0.0)
+    act(a("ptab2", 0, SH), a("gid", 0, SH))
+    act(a("nbu"), a("nbi"), bias=float(SH))
+    act(a("idb"), a("zsl", 16, 144))
+    act(a("idf"), a("zsl", 16, 144))
     act(a("zz"), a("jm"), scale=0.0)
     for k0, k1, t in PIECES[:-1]:
         act(a("st", 8 + 16 * k0, SH + 16 * k0), a("jm", 0, 8), scale=0.0)
     act(a("numt", 0, SH), a("jm", 0, SH), scale=0.0, bias=64.0)
-    fold16(a("k4", 0, 96), "gsf", "cmk", 0, 1536)
-
-    def decode(q, land, dd, lu, ptab):
-        ts(a(dd), a(land), float(me - 1), Op.max, float(me + C), Op.min)
-        tt(a(lu), a(dd), a("basec"), Op.add)
-        gather(q, a(ptab, G0, TB), a("od"), a(lu))
-
-    decode("s", "land1", "d1", "lu1", "ptab1")
-    tt(a("cs", 256, 384), a("lo", 0, 128), a("lo", 128, 256), Op.max)
-    tt(a("cs", 384, 512), a("lo", 0, 128), a("lo", 128, 256), Op.min)
-    f1b = a("fb", 4 * NG, 5 * NG)
-    tt(f1b, ind(a("ptab1"), a("l1bu")), a("gidb"), Op.not_equal)
-    left2 = send(2, "fb", C, "ftab", G0, 4 * NG)
-    iota(a("yw", V + 1024, 2 * V), [[0, 1024]], 0, 0)
-    dma("y", a("xo"), lambda: T.x[:, :], after=[left2])
-    act(slot("ftab", r, C, G0), slot("fb", r, C, 4 * NG))
-    act(a("k5", 0, NG), f1b, scale=-float(BIG), bias=float(BIG))
-    ts(a("n3i"), a("cs", 0, 384), 4095, Op.bitwise_and)
-    tc(a("codeb"), a("k4", 0, 96))
-    act(a("n3u"), a("n3i"))
-    gather("s", a("wb"), a("w16"), a("blu"))
-    tt(a("ftab", SH, G0), ind(a("ptab1"), a("l1u")), a("gid", SH, G0), Op.not_equal)
-    fold16(a("k0", 0, 128), "hb", "ftab", SH, G0)
+    if r > 0:
+        act(a("st", G0, me), a("gid", G0, me), scale=0.0)
+    if r < 7:
+        act(a("numg", low, NG), a("gid", me + C, TB), scale=0.0, bias=64.0)
+    gather("s", a("wb", 0, low), a("w16"), a("blu", 0, low // 16))
+    for h in (0, 1):
+        c = SH + 1024 * h
+        tt(a("ftab", c, c + 1024), ind(a("ptab1"), a("l1u", 64 * h, 64 * h + 64)), a("gid", c, c + 1024), Op.not_equal)
+        fold16(a("k0", 64 * h, 64 * h + 64), "hb", "ftab", c, c + 1024)
+    ts(a("codeb"), a("k4", 0, 96), float(TOP), Op.add)
     ts(a("nbba"), a("codeb"), 4095, Op.bitwise_and)
-    act(a("sc1"), a("mc", 1, 2), scale=-1.0, bias=1.0)
-    act(a("bi1"), a("mc", 1, 2), scale=float(r + 1), bias=-1.0)
-    act(a("pS"), a("cf"), scale=2047.0, bias=1.0)
     tc(a("nbbu"), a("nbba"))
-    tt(a("gq"), a("gidb"), a("k5", 0, NG), Op.max)
+    ts(a("n3i"), a("cs", 0, 384), 4095, Op.bitwise_and)
+    act(a("n3u"), a("n3i"))
+    ts(a("m1bl"), a("k5", 0, 24), -1.0, Op.mult, 1.0, Op.add)
+    ts(a("m1B"), a("k0", 0, 128), -1.0, Op.mult, 1.0, Op.add)
+    tt(a("keepb"), a("q1b"), a("m1bl"), Op.mult)
+    tt(a("keep"), a("q1"), a("m1B"), Op.mult)
 
     gather("s", a("fb", 0, 768), a("ftab"), a("nbbu", 0, 48))
     gather("v", a("fb", 768, 1536), a("ftab"), a("nbbu", 48, 96))
-    fold16(a("k1", 0, 120), "hb", "fb", 0, 5 * NG)
+    fold16(a("k1", 0, 96), "hb", "fb", 0, 4 * NG)
 
     def flags(q, d, h, k0=0, k1=64):
         c, k = 1024 * (2 * d + h), 128 * d + 64 * h
@@ -370,35 +402,35 @@ def rank_program(g, core, T, topo):
 
     flags("s", 0, 0)
     flagfold(0, 0)
-    flags("v", 2, 0)
-    flagfold(2, 0)
+    for h in (0, 1):
+        tt(a("key", 256 * h + 192, 256 * h + 256), a("cs", 384 + 64 * h, 448 + 64 * h), a("keep", 64 * h, 64 * h + 64), Op.max)
+    flags("v", 2, 0, 0, 24)
     tt(a("kb"), a("codeb"), a("k1", 0, 96), Op.mult)
     tt(a("h2b"), a("kb", 0, 48), a("kb", 48, 96), Op.max)
-    tt(a("q2b"), a("h2b", 0, 24), a("h2b", 24, 48), Op.max)
+    tt(a("h3b"), a("h2b", 0, 24), a("h2b", 24, 48), Op.max)
+    tt(a("q2b"), a("h3b"), a("keepb"), Op.max)
     ts(a("l2bi"), a("q2b"), 4095, Op.bitwise_and)
-    tt(a("l2b"), a("l2bi"), a("k1", 96, 120), Op.mult)
-    left3 = send(3, "l2b", 3, "land2")
+    encode("out2", "d2", a("l2bi"), "rel2")
+    left3 = send(3, "out2", 3, "lu2")
+    iota(a("numt", SH, G0), [[0, V]], r, 0)
+    flags("v", 2, 0, 24, 64)
+    flagfold(2, 0)
     for c in range(16):
         dma("y", a("wa", p0=c, ps=16), lambda: T.w[:, 0:2 * V], after=[left3])
-    ts(a("m1bl"), a("k1", 96, 120), -1.0, Op.mult, 1.0, Op.add)
-    tc(a("l2bu"), a("l2b"))
-    tc(a("se2", 0, 3), slot("l2b", r, 3))
-    tt(a("l1mb"), a("m1bl"), a("l1b"), Op.mult)
     flags("s", 1, 0)
+    act(a("l2bu"), a("l2bi"))
+    act(a("se2", 0, 3), slot("l2bi", r, 3))
     flagfold(1, 0)
-    tt(a("candu"), a("l1mb"), a("l2b"), Op.add)
     flags("s", 0, 1)
     flagfold(0, 1)
 
     def pointers(h):
         k, c = "k%d" % (2 + h), 64 * h
-        for d in range(3):
-            tt(a("key", 192 * h + 64 * d, 192 * h + 64 * d + 64), a("cs", 128 * d + c, 128 * d + c + 64), a(k, 64 * d, 64 * d + 64), Op.mult)
-        tt(a("h2", 2 * c, 2 * c + 64), a("key", 192 * h, 192 * h + 64), a("key", 192 * h + 64, 192 * h + 128), Op.max)
-        tt(a("h2", 2 * c + 64, 2 * c + 128), a("key", 192 * h + 128, 192 * h + 192), a("cs", 384 + c, 448 + c), Op.max)
+        tt(a("key", 4 * c, 4 * c + 192), a("csh", 3 * c, 3 * c + 192), a(k, 0, 192), Op.mult)
+        tt(a("h2", 2 * c, 2 * c + 128), a("key", 4 * c, 4 * c + 128), a("key", 4 * c + 128, 4 * c + 256), Op.max)
         tt(a("q2", c, c + 64), a("h2", 2 * c, 2 * c + 64), a("h2", 2 * c + 64, 2 * c + 128), Op.max)
         ts(a("l2i", c, c + 64), a("q2", c, c + 64), 4095, Op.bitwise_and)
-        tt(a("l2u", c, c + 64), a("l2i", c, c + 64), a("k0", c, c + 64), Op.mult)
+        tc(a("l2u", c, c + 64), a("l2i", c, c + 64))
 
     flags("v", 2, 1)
     flagfold(2, 1)
@@ -407,135 +439,138 @@ def rank_program(g, core, T, topo):
     flags("v", 1, 1, 40, 64)
     flagfold(1, 1)
     gather("s", a("od", 50 * r + 1, 50 * r + 49), a("gid"), a("se2", 0, 3))
-    gather("s", a("yc"), a("xw"), a("candu"))
+    gather("s", a("yc"), a("xw"), a("l2bu"))
     gather("v", a("ptab2", SH, SH + 384), a("gid"), a("l2u", 0, 24))
     gather("s", a("ptab2", SH + 384, SH + 1024), a("gid"), a("l2u", 24, 64))
     pointers(1)
-    decode("s", "land2", "d2", "lu2", "ptab2")
-    gather("v", a("ptab2", SH + 1024, SH + 1664), a("gid"), a("l2u", 64, 104))
-    gather("s", a("ptab2", SH + 1664, G0), a("gid"), a("l2u", 104, 128))
-    act(a("k4", 0, NG), a("yc"))
-    act(a("m1B"), a("k0", 0, 128), scale=-1.0, bias=1.0)
-    tt(a("m2b"), ind(a("ptab2"), a("l2bu")), a("gq"), Op.is_equal)
+    mm(a("k4", 0, NG), a("idb"), a("yc"))
+    gather("v", a("ptab2", SH + 1024, SH + 1792), a("gid"), a("l2u", 64, 112))
+    gather("s", a("ptab2", SH + 1792, G0), a("gid"), a("l2u", 112, 128))
+    gather("s", a("ptab2", G0, TB), a("od"), a("lu2"))
+    tt(a("m2b"), ind(a("ptab2"), a("l2bu")), a("gidb"), Op.is_equal)
     tt(a("xmb"), a("m2b"), a("k4", 0, NG), Op.mult)
     send(4, "xmb", C, "xm")
+    for c in range(16):
+        mm(a("k0", c, 128, 16), a("ptab2", SH + c, G0, 16), a("hf", 16, 144, 16))
     gather("s", a("pp2", 0, 1024), a("ptab2"), a("l2u", 0, 64))
     fold16(a("k6", 0, 64), "hh", "pp2", 0, 1024)
-    gather("v", a("pp2", 1024, 1536), a("ptab2"), a("l2u", 64, 96))
-    gather("s", a("pp2", 1536, 2048), a("ptab2"), a("l2u", 96, 128))
+    gather("v", a("pp2", 1024, 1664), a("ptab2"), a("l2u", 64, 104))
+    gather("s", a("pp2", 1664, 2048), a("ptab2"), a("l2u", 104, 128))
     fold16(a("k7", 0, 64), "hh", "pp2", 1024, 2048)
-    tt(a("l1m"), a("m1B"), a("l1f"), Op.mult)
 
     def mates(h):
         c = 64 * h
         tt(a("m2B", c, c + 64), a("k%d" % (6 + h), 0, 64), a("vB", c, c + 64), Op.is_equal)
-        tt(a("m2l", c, c + 64), a("m2B", c, c + 64), a("l2i", c, c + 64), Op.mult)
-        tt(a("mu", c, c + 64), a("m2l", c, c + 64), a("l1m", c, c + 64), Op.max)
+        tt(a("mu", c, c + 64), a("m2B", c, c + 64), a("l2i", c, c + 64), Op.mult)
 
-    def features(h):
-        c = 1024 * h
-        tt(a("xt", SH + c, SH + c + 1024), ind(a("xw"), a("mu", 64 * h, 64 * h + 64)), a("xo", c, c + 1024), Op.add)
-
-    def mates_names(k0, k1):
-        gather("s", a("mg", 16 * k0, 16 * k1), a("gid"), a("mu", k0, k1))
-
+    ts(a("pZ"), a("cf"), 1.0, Op.is_gt, 1000.0, Op.mult)
+    ts(a("pS"), a("cf"), 2047.0, Op.mult, 1.0, Op.add)
+    tt(a("gtc"), a("k0", 0, 128), a("vT"), Op.is_gt)
+    tt(a("pY"), a("pZ"), a("p16"), Op.add)
     mates(0)
+    ts(a("hh2"), a("jj", 0, 144), a("pY"), Op.is_equal, a("pS"), Op.mult)
+    mm(a("k0", 0, 128), a("gtc"), a("idb"))
     act(slot("xm", r, C), slot("xmb", r, C))
-    features(0)
-    mates_names(0, 64)
-    fold16(a("k2", 0, 64), "hh", "mg", 0, 1024)
+    gather("s", a("xg"), a("xw"), a("mu", 0, XS // 16))
     mates(1)
+    tt(a("rep"), a("k0", 0, 128), a("m2B"), Op.is_ge)
+    mm(a("k0", 0, 128), a("gb"), a("rep"))
+    mm(a("k0", 128, 256), a("tri"), a("rep"))
+    for c in range(0, XS, 512):
+        k, e = a("k%d" % (2 + c // 512), 0, min(512, XS - c)), min(XS, c + 512)
+        mm(k, a("idb"), a("xo", c, e), True, False)
+        mm(k, a("idb"), a("xg", c, e), False, True)
+        act(a("xt", SH + c, SH + e), k)
+    tt(a("xt", SH + XS, G0), ind(a("xw"), a("mu", XS // 16, 128)), a("xo", XS, V), Op.add)
+    for k0, k1, t in PIECES:
+        act(a("mur", k0, k1), a("mu", k0, k1), bias=-float(8 + 16 * k0), func=Fn.Relu)
+    mm(a("k1", 0, NG), a("idb"), a("xw", G0, TB))
     for d in range(D):
-        mm(a("k%d" % (4 + d), 0, NG), a("sel", 128 * d, 128 * d + 128), a("wb"))
-    mm(a("k1", 0, NG), a("idb"), a("xw", G0, TB), True, False)
-    mm(a("k1", 0, NG), a("idb"), a("xm"), False, True)
-    features(1)
-    mates_names(64, 96)
-    act(a("xt", G0, TB), a("k1", 0, NG))
-    mates_names(96, 128)
-    fold16(a("k2", 64, 128), "hh", "mg", 1024, 2048)
+        mm(a("k%d" % (4 + d), 0, low), a("sel", 128 * d, 128 * d + 128), a("wb", 0, low))
+    op("v", lambda: g.vector.tensor_tensor_scan(ap(a("sc")), ap(a("k0", 0, 128)), ap(a("zz")), 0.0, Op.add, Op.add),
+       [a("sc")], [a("k0", 0, 128), a("zz")])
+    tt(a("nin"), a("sc"), a("k0", 128, 256), Op.add)
+    mm(a("k0", 0, 128), a("nin"), a("zsl", 16, 144))
+    act(a("ninT"), a("k0", 0, 128), bias=-1.0)
+    for gr in range(8):
+        dma("y", a("numt", SH, G0, p0=16 * gr, p1=16 * gr + 1), a("ninT", 16 * gr, 16 * gr + 16))
+    act(a("na"), a("nin"), bias=float(V - 1))
+    act(a("numf"), a("nin"), bias=float(V * r - 1))
+    tt(a("xt", G0, TB), a("k1", 0, NG), a("xm"), Op.add)
 
     def near(i):
         k0, k1, t = PIECES[i]
-        for d in (0, 1):
+        for d in range(NEAR[i]):
             tt(a("pr", V * d + 16 * k0, V * d + 16 * k1), ind(a("xt"), a("nbu", 128 * d + k0, 128 * d + k1)),
                a("wa", V * d + 16 * k0, V * d + 16 * k1), Op.mult)
+        if JOIN[i]:
+            x, y = a("pr", 16 * k0, 16 * k1), a("pr", V + 16 * k0, V + 16 * k1)
+            op("g", lambda: g.dma_start(out=ap(x), in_=ap(y), accum_op=Op.add), [x], [x, y], inc=16)
 
     def wcast(i):
         k0, k1, t = PIECES[i]
-        for d in (2, 3):
-            mm(a("k%d" % (2 + d + 2 * (i % 2)), 0, 16 * (k1 - k0)), a("sel", 128 * d, 128 * d + 128), a("w16", 16 * k0, 16 * k1))
+        for d in range(NEAR[i], D):
+            mm(a(BANKS[i][d], 0, 16 * (k1 - k0)), a("sel", 128 * d, 128 * d + 128), a("w16", 16 * k0, 16 * k1))
 
     def gather23(i):
         k0, k1, t = PIECES[i]
-        for d in (2, 3):
+        for d in range(NEAR[i], D):
             gather("s", a("pr", V * d + 16 * k0, V * d + 16 * k1), a("xt"), a("nbu", 128 * d + k0, 128 * d + k1))
 
     def far(i):
         k0, k1, t = PIECES[i]
-        n = 16 * (k1 - k0)
         p = [a("pr", V * d + 16 * k0, V * d + 16 * k1) for d in range(D)]
-        w2, w3 = [a("k%d" % (2 + d + 2 * (i % 2)), 0, n) for d in (2, 3)]
+        k = a(BANKS[i][0], 0, 16 * (k1 - k0))
         out = a("st", SH + 16 * k0, SH + 16 * k1)
-        if t == 0:
-            tt(w2, p[2], w2, Op.mult)
-            tt(p[3], p[3], w3, Op.mult)
-            tt(w2, p[0], w2, Op.add)
-            tt(w2, p[1], w2, Op.add)
-            return lambda: tt(out, p[3], w2, Op.add)
-        k = a("k%d" % (i % 2), 0, n)
-        tt(p[2], p[2], w2, Op.mult)
-        tt(p[3], p[3], w3, Op.mult)
+        for d in range(NEAR[i], D):
+            tt(p[d], p[d], a(BANKS[i][d], 0, 16 * (k1 - k0)), Op.mult)
+        if JOIN[i]:
+            p = p[2:] + p[:1]
         for d in range(t):
             mm(k, a("idf"), p[d], d == 0, d == t - 1)
-        if t == 3:
-            return lambda: tt(out, p[3], k, Op.add)
-        return lambda: act(out, k)
 
-    near(0)
-    for d in range(D):
-        gather("s", a("cmk", NG * d, NG * d + NG), a("xt"), a("nbbu", 24 * d, 24 * d + 24))
-    tt(a("rep"), a("k2", 0, 128), a("vB"), Op.is_gt)
-    mm(a("k2", 0, 128), a("gb"), a("rep"))
-    mm(a("k3", 0, 128), a("tri"), a("rep"))
-    b = [a("cmk", NG * d, NG * d + NG) for d in range(D)]
-    w = [a("k%d" % (4 + d), 0, NG) for d in range(D)]
-    tt(w[0], b[0], w[0], Op.mult)
-    tt(b[1], b[1], w[1], Op.mult)
-    op("v", lambda: g.vector.tensor_tensor_scan(ap(a("sc")), ap(a("k2", 0, 128)), ap(a("zz")), 0.0, Op.add, Op.add),
-       [a("sc")], [a("k2", 0, 128), a("zz")])
-    tt(w[0], b[1], w[0], Op.add)
-    tt(a("nin"), a("sc"), a("k3", 0, 128), Op.add)
-    for bk in range(4):
-        for c in range(16):
-            mm(a("k%d" % bk, c, 512, 16), a("zsl", 16 + c, 144 + c), a("nin", 32 * bk, 32 * bk + 32))
-    tt(b[2], b[2], w[2], Op.mult)
-    tt(w[0], b[2], w[0], Op.add)
-    tt(b[3], b[3], w[3], Op.mult)
-    tt(a("sb"), b[3], w[0], Op.add)
-    send(5, "sb", C, "st", G0)
+        def rest():
+            for x in p[t:-1]:
+                tt(k, x, k, Op.add)
+            if t < len(p):
+                tt(out, p[-1], k, Op.add)
+            else:
+                act(out, k)
+        return rest
+
     wcast(0)
+    near(0)
     gather23(0)
-    wcast(1)
-    near(1)
-    for bk in range(4):
-        act(a("numt", SH + 512 * bk, SH + 512 * bk + 512), a("k%d" % bk), scale=a("sc1"), bias=a("bi1"))
-        if bk == 1:
-            act(slot("st", r, C, G0), slot("sb", r, C))
-            act(a("na"), a("nin"), bias=float(V - 1))
-            gather23(1)
     end0 = far(0)
-    gather("s", a("numb"), a("numt", SH, G0), a("blu"))
-    send(6, "numb", C, "numt", G0)
-    wcast(2)
-    end1 = far(1)
-    gather23(2)
-    act(a("numf"), a("nin"), bias=float(V * r - 1))
-    act(slot("numt", r, C, G0), slot("numb", r, C))
+    for d in range(D):
+        gather("s", a("cmk", NG * d, NG * d + low), a("xt"), a("nbbu", 24 * d, 24 * d + low // 16))
+    b = [a("cmk", NG * d, NG * d + low) for d in range(D)]
+    w = [a("k%d" % (4 + d), 0, low) for d in range(D)]
+    tt(w[0], b[0], w[0], Op.mult)
     tt(a("nm"), a("na"), a("rep"), Op.mult)
-    for k0, k1, t in PIECES:
-        ts(a("mur", k0, k1), a("mu", k0, k1), -float(8 + 16 * k0), Op.add, 0.0, Op.max)
+    tt(b[1], b[1], w[1], Op.mult)
     tt(a("posu"), a("nm"), a("vB"), Op.max)
+    tt(w[0], b[1], w[0], Op.add)
+    tt(b[2], b[2], w[2], Op.mult)
+    tt(b[3], b[3], w[3], Op.mult)
+    tt(w[0], b[2], w[0], Op.add)
+    tt(a("sb", 0, low), b[3], w[0], Op.add)
+    send(5, "sb", C, "st", G0)
+    wcast(1)
+    wcast(2)
+    gather23(1)
+    near(1)
+    end1 = far(1)
+    wcast(3)
+    gather23(2)
+    gather("s", a("numb", high, NG), a("numt", SH, G0), a("blu", high // 16, 24))
+    send(6, "numb", C, "numg")
+    near(2)
+    end0()
+    gather23(3)
+    act(slot("st", r, C, G0), slot("sb", r, C))
+    end2 = far(2)
+    near(3)
     last = []
 
     def mates_sums(i):
@@ -543,39 +578,33 @@ def rank_program(g, core, T, topo):
         for c1, c0 in zip(CUTS[i], CUTS[i][1:]):
             gather("s", a("g2", 16 * c0, 16 * c1), a("st", 8 + 16 * k0, TB), a("mur", c0, c1))
 
-    def scatter(i):
-        for c1, c0 in zip(CUTS[i], CUTS[i][1:]):
+    def scatter(i, part=None):
+        cuts = CUTS[i] if part is None else CUTS[i][part:part + 2]
+        for c1, c0 in zip(cuts, cuts[1:]):
             tt(ind(a("yw", 0, V + 16 * c1), a("posu", c0, c1)), a("st", SH + 16 * c0, SH + 16 * c1), a("g2", 16 * c0, 16 * c1), Op.add)
             last.append(dma("y", (lambda c0, c1: lambda: T.y[:, c0:c1])(16 * c0, 16 * c1), a("yw", V + 16 * c0, V + 16 * c1)))
 
     def mates_numbers(h):
         gather("s", a("nmate", 1024 * h, 1024 * h + 1024), a("numt"), a("mu", 64 * h, 64 * h + 64))
-        fold16(a("k2", 64 * h, 64 * h + 64), "hh2", "nmate", 1024 * h, 1024 * h + 1024)
+        fold16(a("k7", 64 * h, 64 * h + 64), "hh2", "nmate", 1024 * h, 1024 * h + 1024)
 
-    near(2)
-    end0()
-    wcast(3)
-    gather23(3)
-    end2 = far(2)
+    act(slot("numg", r, C), slot("numb", r, C))
     mates_sums(0)
-    ts(a("pZ"), a("cf"), 1.0, Op.is_gt, 1000.0, Op.mult)
-    near(3)
     end1()
-    tt(a("pY"), a("pZ"), a("p16"), Op.add)
-    mates_sums(1)
     end3 = far(3)
-    ts(a("hh2"), a("jj", 0, 144), a("pY"), Op.is_equal, a("pS"), Op.mult)
+    mates_sums(1)
+    act(a("numt", G0, TB), a("numg"))
     mates_numbers(0)
     scatter(0)
     end2()
     mates_sums(2)
+    mates_numbers(1)
     scatter(1)
     end3()
-    mates_numbers(1)
     mates_sums(3)
     scatter(2)
-    tt(a("cmo"), a("k2", 0, 128), a("numf"), Op.min)
-    last.append(dma("y", lambda: T.cm[:, :], a("cmo")))
+    tt(a("cmo"), a("k7", 0, 128), a("numf"), Op.min)
+    last.append(dma("s", lambda: T.cm[:, :], a("cmo")))
     scatter(3)
     ops.append({"q": "y", "fn": None, "dep": set(last), "inc": 0, "sem": None, "waits": [], "K": 0})
 
@@ -623,5 +652,6 @@ def rank_program(g, core, T, topo):
             x = o["fn"]()
             if i in where:
                 x.then_inc(T.sem[where[i]], o["inc"])
-    for k in range(7):
-        g.wait_ge(T.sem["t%d" % k], engines)
+    for k in range(8):
+        if engines[k]:
+            g.wait_ge(T.sem["t%d" % k], engines[k])

from concourse.bass import DstId, RemoteDMATransfer
from concourse.mybir import AluOpType as Op, ActivationFunctionType as Fn

N, V, D, C = 8, 2048, 4, 48
NG = N * C
SH = 16
G0 = SH + V
TB = G0 + NG
TOP = 3 * 4096 + 1024
BIG = 4096
PIECES = ((96, 128, 4), (64, 96, 3), (32, 64, 3), (0, 32, 3))
NEARS = ((2, 2, 2, 2), (2, 2, 2, 2))
JOIN = (0, 0, 0, 0)
BANKS = (("k1", "k0", "k2", "k3"), ("k0", "k7", "k2", "k3"), ("k1", "k4", "k5", "k6"), ("k5", "k7", "k2", "k3"))
XS = 768
CUTS = ((128, 96), (96, 64), (64, 32), (32, 12, 0))

_F, _B, _I, _H, _U = "float32", "bfloat16", "int32", "float16", "uint16"
_LOG = {n: (w, t) for n, w, t in [
    ("pf", 1, _F), ("pi", 1, _I), ("ci", 1, _I), ("cf", 1, _F), ("c1000", 1, _F), ("p16", 1, _F), ("pX", 1, _F),
    ("pY", 1, _F), ("pZ", 1, _F), ("pS", 1, _F), ("hh2", 144, _H), ("ninT", 128, _F),
    ("u32", 32, _F), ("ee", 32, _B), ("dm", 48, _B),
    ("jj", 160, _F), ("jm", 128, _F), ("v16", 128, _F), ("vB", 128, _F), ("rel1", 24, _F), ("rel2", 24, _F), ("selfc", 3, _U),
    ("mc", 16, _F), ("idb", 128, _B), ("idf", 128, _F), ("ip", 128, _B), ("inn", 128, _B), ("zsl", 160, _H), ("gsh", 144, _H),
    ("gsf", 144, _F), ("hb", 144, _B), ("hh", 144, _H), ("hf", 144, _F), ("gb", 128, _B), ("tri0", 128, _B), ("tri", 128, _B),
    ("sel", 512, _B), ("zz", 128, _F), ("gid", TB, _F), ("od", 400, _F),
    ("wr", V, _B), ("w16", V, _B), ("nbi", 512, _I), ("bli", 24, _I), ("xw", TB, _B), ("xo", V, _B), ("wa", 2 * V, _B),
    ("nbu", 512, _U), ("ones", 128, _H), ("base", 512, _H), ("blu", 24, _U), ("blh", 24, _I), ("blx", 24, _U), ("bll", 24, _I), ("blo", 24, _U),
    ("gidb", NG, _F), ("mask", NG, _F), ("xb", NG, _B),
    ("gt", 768, _B), ("code", 512, _F), ("cs", 512, _I), ("hi", 512, _F), ("lo", 256, _F), ("q1", 128, _F), ("l1u", 128, _U), ("n3i", 384, _I),
    ("n3u", 384, _U), ("l1s", 128, _F), ("l1f", 128, _F), ("lm", NG, _H), ("l1b", 24, _F), ("l1bu", 24, _U), ("csh", 384, _F),
    ("d1", 24, _F), ("out1", 24, _U), ("lu1", 24, _U), ("se1", 4, _U), ("ptab1", TB, _F), ("ftab", TB, _B),
    ("f1b", NG, _B), ("m1B", 128, _F), ("keep", 128, _F), ("q1b", 24, _F), ("m1bl", 24, _F), ("keepb", 24, _F),
    ("cmk", 1536, _F), ("codeb", 96, _I), ("nbba", 96, _I), ("nbbu", 96, _U), ("wb", NG, _B),
    ("fb", 4 * NG, _B), ("kb", 96, _F), ("h2b", 48, _F), ("h3b", 24, _F), ("q2b", 24, _I), ("l2bi", 24, _I), ("l2bu", 24, _U),
    ("yc", NG, _B), ("fl", 3 * V, _B), ("key", 512, _F), ("h2", 256, _F), ("q2", 128, _I), ("l2i", 128, _I), ("l2u", 128, _U),
    ("out2", 24, _U), ("d2", 24, _F), ("lu2", 24, _U), ("se2", 4, _U), ("ptab2", TB, _F),
    ("m2b", NG, _B), ("xmb", NG, _B), ("xm", NG, _B), ("xg", XS, _B),
    ("pp2", V, _H), ("m2B", 128, _F), ("mu", 128, _U), ("mur", 128, _U),
    ("gtc", 128, _B), ("vT", 128, _F), ("rep", 128, _B), ("sc", 128, _F), ("nin", 128, _H), ("na", 128, _F), ("nm", 128, _F),
    ("numf", 128, _F), ("posu", 128, _U), ("numt", TB, _F), ("numb", NG, _H), ("numg", NG, _H), ("nmate", V, _H), ("cmo", 128, _F),
    ("xt", TB, _F), ("sb", NG, _F), ("st", TB, _F), ("pr", 4 * V, _F), ("g2", V, _F), ("yw", 2 * V, _F),
]}
_WHERE, SCRATCH, _fill = {}, {}, {}
for _n, (_w, _t) in _LOG.items():
    if _w <= 512:
        _WHERE[_n] = ("pack_" + _t, _fill.get(_t, 0))
        _fill[_t] = _fill.get(_t, 0) + (_w + 15) // 16 * 16
    else:
        _WHERE[_n] = (_n, 0)
        SCRATCH[_n] = ("sbuf", [128, _w], _t)
for _t, _w in _fill.items():
    SCRATCH["pack_" + _t] = ("sbuf", [128, _w], _t)
_PSUM = {"k%d" % _i: 512 for _i in range(8)}
for _n, _w in _PSUM.items():
    SCRATCH[_n] = ("psum", [128, _w], _F)
    _WHERE[_n] = (_n, 0)
    _LOG[_n] = (_w, _F)
NPOOL = 130
SEMAPHORES = ["e%d" % k for k in range(8)] + ["t%d" % k for k in range(8)] + ["s%d" % i for i in range(NPOOL)]


def a(name, c0=0, c1=None, cs=1, p0=0, p1=128, ps=1):
    return (name, c0, _LOG[name][0] if c1 is None else c1, cs, p0, p1, ps)


def ind(win, off):
    return ("ind", win, off)


def _clash(s, t):
    if s[0] != t[0]:
        return False
    if not (s[1] < t[2] and t[1] < s[2] and s[4] < t[5] and t[4] < s[5]):
        return False
    if s[3] == t[3] > 1 and (s[1] - t[1]) % s[3]:
        return False
    if s[6] == t[6] > 1 and (s[4] - t[4]) % s[6]:
        return False
    return True


def _plan(src, topo, dsts):
    used, out = set(), {}
    for far in (True, False):
        todo = [dst for dst in dsts if (topo.chip(dst) != topo.chip(src)) == far]
        for i, dst in enumerate(todo):
            free = [x for x in topo.engines(src, dst) if x not in used]
            n = 1 << ((len(free) // (len(todo) - i)).bit_length() - 1)
            used.update(free[:n])
            out[dst] = free[:n]
    return out


def _targets(k, q, chips):
    if k in (0, 7):
        return [p for p in range(N) if p != q and (chips[p] == chips[q]) == (k == 0)]
    return range(q) if k == 5 else range(q + 1, N) if k == 6 else [p for p in range(N) if p != q]


def rank_program(g, core, T, topo):
    r = T.rank_of(core)
    if r is None:
        return
    ops, acc = [], {}
    mmgroup = {}
    NEAR = NEARS[r * len(NEARS) // N]
    eng = {"v": g.vector, "s": g.scalar, "t": g.tensor, "g": g, "y": g.sync}

    def ap(s):
        if isinstance(s, tuple):
            if s[0] == "ind":
                return ap(s[1]).indirect(ap(s[2]))
            name, b = _WHERE[s[0]]
            cols = slice(b + s[1], b + s[2], s[3]) if s[3] > 1 else slice(b + s[1], b + s[2])
            return T[name][slice(s[4], s[5], s[6]) if s[6] > 1 else slice(s[4], s[5]), cols]
        return s

    def regs(xs):
        out = []
        for s in xs:
            if isinstance(s, tuple):
                out += [s[1], s[2]] if s[0] == "ind" else [s]
        return out

    def op(q, fn, outs, ins, inc=1, stop=None, after=()):
        i = len(ops)
        wr, rd = [], regs(ins)
        for o in outs:
            if o[0] == "ind":
                wr.append(o[1])
                rd.append(o[2])
            else:
                wr.append(o)
        dep = set(after)
        for lst, w in ((rd, False), (wr, True)):
            for s in lst:
                for j, jw, t in acc.get(s[0], ()):
                    if q == "t" and ops[j]["q"] == "t":
                        continue
                    if (s[0] in _PSUM and ops[j]["q"] != q) or ((w or jw) and _clash(s, t)):
                        dep.add(j)
        for lst, w in ((rd, False), (wr, True)):
            for s in lst:
                acc.setdefault(s[0], []).append((i, w, s))
        ops.append({"q": q, "fn": fn, "dep": dep, "inc": inc, "sem": None, "waits": [], "K": 0})
        if q == "t":
            mmgroup.setdefault("open", []).append(i)
            if stop:
                for j in mmgroup["open"]:
                    mmgroup[j] = i
                mmgroup["open"] = []
        return i

    def tt(out, x, y, o):
        op("v", lambda: g.vector.tensor_tensor(out=ap(out), in0=ap(x), in1=ap(y), op=o), [out], [x, y])

    def ts(out, x, s1, o1, s2=None, o2=None):
        if o2 is None:
            op("v", lambda: g.vector.tensor_scalar(out=ap(out), in0=ap(x), scalar1=ap(s1), scalar2=None, op0=o1), [out], [x, s1])
        else:
            op("v", lambda: g.vector.tensor_scalar(out=ap(out), in0=ap(x), scalar1=ap(s1), scalar2=ap(s2), op0=o1, op1=o2),
               [out], [x, s1, s2])

    def tc(out, x):
        op("v", lambda: g.vector.tensor_copy(out=ap(out), in_=ap(x)), [out], [x])

    def ms(out, c):
        op("v", lambda: g.vector.memset(ap(out), c), [out], [])

    def act(out, x, scale=1.0, bias=None, func=Fn.Identity):
        if bias is None:
            op("s", lambda: g.scalar.activation(out=ap(out), in_=ap(x), func=Fn.Copy, scale=ap(scale)), [out], [x, scale])
        else:
            op("s", lambda: g.scalar.activation(out=ap(out), in_=ap(x), func=func, bias=ap(bias), scale=ap(scale)),
               [out], [x, scale, bias])

    def gather(q, out, win, off):
        (tc if q == "v" else act)(out, ind(win, off))

    def mm(out, l, rr, start=True, stop=True, signal=False):
        op("t", lambda: g.tensor.matmul(ap(out), ap(l), ap(rr), start, stop), [out], [l, rr], stop=stop or signal)

    def iota(out, pattern, base, cm):
        if _LOG[out[0]][1] != _I:
            op("g", lambda: g.iota(ap(out), pattern, base, cm, allow_small_or_imprecise_dtypes=True), [out], [])
        else:
            op("g", lambda: g.iota(ap(out), pattern, base, cm), [out], [])

    def dma(q, out, x, after=()):
        f = lambda s: ap(s) if isinstance(s, tuple) else s()
        return op(q, lambda: eng[q].dma_start(out=f(out), in_=f(x)), [out] if isinstance(out, tuple) else [], regs([x]), inc=16,
                  after=after)

    def _to(k, q):
        return _targets(k, q, [topo.chip(c) for c in T.cores])

    plans = [[_plan(T.cores[q], topo, [T.cores[p] for p in _to(k, q)]) for q in range(N)] for k in range(8)]
    engines = [sum(len(e) for e in plans[k][r].values()) for k in range(8)]

    def slot(name, q, w, base=0):
        return a(name, base + w * q, base + w * q + w)

    def event(sem, count):
        ops.append({"q": "r", "fn": None, "dep": set(), "inc": count, "sem": sem, "waits": [], "K": 0})
        return len(ops) - 1

    def arrive(k, name, w, base=0):
        for q in range(N):
            if r in _to(k, q):
                acc.setdefault(name, []).append((len(ops), True, slot(name, q, w, base)))
        event("e%d" % k, sum(len(plans[k][q].get(core, ())) for q in range(N)))

    def send(k, name, w, dname, base=0, sbase=0):
        dst = slot(dname, r, w, base)

        def fn():
            tr = []
            for q in _to(k, r):
                rid, pid, _se = topo.addr(T.cores[q])
                tr.append(RemoteDMATransfer(dst_ids=[DstId(rid=rid, pnc=pid)], dma_engine_mask=sum(1 << e for e in plans[k][r][T.cores[q]]),
                                            remote_sem=T.sem["e%d" % k], src=ap(slot(name, q, w, sbase)), dst=ap(dst)))
            g.remote_dma_fused(tr, local_sem=T.sem["t%d" % k])
        if engines[k]:
            op("g", fn, [], [slot(name, q, w, sbase) for q in _to(k, r)])
        return event("t%d" % k, engines[k])

    def fold16(out, lhs, name, c0, c1):
        for c in range(16):
            mm(out, a(lhs, 16 - c, 144 - c), a(name, c0 + c, c1, 16), c == 0, c == 15)

    for k, name, w, base in ((0, "xw", C, G0), (1, "lu1", 3, 0), (2, "ftab", C, G0), (3, "lu2", 3, 0), (4, "xm", C, 0),
                             (5, "st", C, G0), (6, "numg", C, 0), (7, "xw", C, G0)):
        arrive(k, name, w, base)
    me = G0 + C * r
    low, high = C * (r + 1), C * (r - r % 2)

    dma("y", a("wr", p1=32), lambda: T.w[:, :])
    dma("s", a("bli"), lambda: T.bl[:, :])
    dma("y", a("xw", SH, G0), lambda: T.x[:, :])
    dma("y", a("nbi"), lambda: T.nb[:, :])
    iota(a("u32"), [[1, 4], [4, 8]], 0, -1)
    iota(a("pf"), [[1, 1]], 0, 1)
    iota(a("pi"), [[1, 1]], 0, 1)
    iota(a("jj"), [[1, 160]], -16, 0)
    iota(a("jm"), [[16, 8], [0, 16]], 0, 0)
    iota(a("gid", SH, SH + 512), [[1, 512]], 0, 0)
    iota(a("v16"), [[16, 128]], 0, 0)
    iota(a("rel1"), [[-C, 8], [0, 3]], 50 * r + 1 - G0 + 1024, 0)
    iota(a("rel2"), [[-C, 8], [0, 3]], 50 * r + 1 - G0, 0)
    ms(a("od"), float(BIG))
    ts(a("ee"), a("u32"), 0.0, Op.is_equal)
    tt(a("dm", 0, 24), a("ee", 8, 32), a("ee", 0, 24), Op.subtract)
    tt(a("dm", 24, 40), a("ee", 16, 32), a("ee", 0, 16), Op.subtract)
    tt(a("dm", 40, 48), a("ee", 24, 32), a("ee", 0, 8), Op.subtract)
    ts(a("ci"), a("pi"), 15, Op.bitwise_and)
    ms(a("gid", 0, SH), float(BIG))
    tc(a("cf"), a("ci"))
    if r > 0:
        ms(a("gid", G0, me), -1.0)
    if r < 7:
        ms(a("gid", me + C, TB), float(BIG))
    ts(a("zsl"), a("jj"), a("pf"), Op.is_equal)
    ts(a("mc"), a("jj", 16, 32), a("cf"), Op.is_equal)
    tt(a("p16"), a("pf"), a("cf"), Op.subtract)
    act(a("ip"), a("zsl", 16, 144), scale=4096.0)
    act(a("inn"), a("zsl", 16, 144), scale=-4096.0)
    act(a("ones"), a("zsl", 16, 144), scale=0.0, bias=1.0)
    for d in range(D):
        act(a("base", 128 * d, 128 * d + 128), a("zsl", 16, 144), scale=float(SH + (3 - d) * 4096 - TOP))
    ts(a("gsh"), a("jj", 0, 144), a("p16"), Op.is_equal)
    ts(a("pX"), a("cf"), 1000.0, Op.mult, a("pf"), Op.add)
    ts(a("bll"), a("bli"), 15, Op.bitwise_and)
    ts(a("blh"), a("bli"), 4, Op.logical_shift_right)
    tc(a("blu"), a("bli"))
    tc(a("blo"), a("bll"))
    tc(a("blx"), a("blh"))
    ts(a("hb"), a("jj", 0, 144), a("pX"), Op.is_equal)
    ts(a("gb"), a("jm"), a("p16"), Op.is_equal)
    gather("s", a("mask"), a("mc"), a("blo"))
    act(a("gid", SH + 512, SH + 1024), a("gid", SH, SH + 512), bias=512.0)
    for b in (0, 1):
        for c in range(16):
            mm(a("k%d" % b, c, 384, 16), a("wr", c, V, 16, p1=32), a("dm", 24 * b, 24 * b + 24, p1=32))
    gather("s", a("xb"), a("xw", SH, G0), a("blu"))
    send(0, "xb", C, "xw", G0)
    act(a("gid", SH + 1024, G0), a("gid", SH, SH + 1024), bias=1024.0)
    gather("s", a("gidb"), a("gid", SH, G0), a("blu"))

    ts(a("gt", 0, 384), a("k0", 0, 384), 0.0, Op.is_gt)
    ts(a("gt", 384, 768), a("k1", 0, 384), 0.0, Op.is_gt)
    g01, g12, g23, g02, g13, g03 = [a("gt", 128 * i, 128 * i + 128) for i in range(6)]
    for d, terms in enumerate((((g01, -1), (g02, -1), (g03, -1)), ((g01, 1), (g12, -1), (g13, -1)),
                               ((g12, 1), (g23, -1), (g02, 1)), ((g23, 1), (g13, 1), (g03, 1)))):
        mm(a("k2", 128 * d, 128 * d + 128), a("ones"), a("base", 128 * d, 128 * d + 128), True, False)
        for i, (s, sg) in enumerate(terms):
            mm(a("k2", 128 * d, 128 * d + 128), s, a("ip" if sg > 0 else "inn"), False, i == 2)
    ts(a("selfc"), a("v16", 0, 3), a("cf"), Op.add, float(50 * r + 1), Op.add)
    for land in ("lu1", "lu2"):
        dma("y", slot(land, r, 3), a("selfc"))
    for d in range(D):
        ts(a("sel", 128 * d, 128 * d + 128), a("jm"), float(d), Op.add, a("pf"), Op.is_equal)
    ts(a("tri0"), a("jj", 16, 144), a("pf"), Op.is_lt, -1.0, Op.mult)
    act(slot("gid", r, C, G0), slot("gidb", r, C))
    act(a("gsf"), a("gsh"))
    tt(a("code", 0, 256), a("k2", 0, 256), a("nbi", 0, 256), Op.add)
    tt(a("k1", 0, 256), a("k2", 256, 512), a("nbi", 256, 512), Op.add)
    tt(a("hi", 0, 256), a("code", 0, 256), a("k1", 0, 256), Op.max)
    tt(a("l1s"), a("hi", 0, 128), a("hi", 128, 256), Op.max)
    tt(a("lm"), ind(a("l1s"), a("blx")), a("mask"), Op.mult)
    act(a("l1u"), a("l1s"), bias=1024.0)
    fold16(a("k3", 0, 24), "gsh", "lm", 0, NG)
    tt(a("lo"), a("code", 0, 256), a("k1", 0, 256), Op.min)
    act(a("code", 256, 512), a("k1", 0, 256))
    gather("s", a("ptab1", SH, G0), a("gid"), a("l1u"))

    def encode(out, dd, x, rel):
        tt(a(dd), x, a(rel), Op.add)
        ts(a(out), a(dd), float(50 * r), Op.max, float(50 * r + C + 1), Op.min)

    encode("out1", "d1", a("k3", 0, 24), "rel1")
    left1 = send(1, "out1", 3, "lu1")
    ts(a("l1b"), a("k3", 0, 24), 1024.0, Op.add)
    iota(a("yw", V, V + 1024), [[0, 1024]], 0, 0)
    for c in range(16):
        dma("y", a("w16", p0=c, ps=16), (lambda d: lambda: T.w[:, V * d:V * d + V])(c % D), after=[left1])

    tc(a("l1bu"), a("l1b"))
    tc(a("se1", 0, 3), slot("l1b", r, 3))
    ms(a("ptab1", 0, SH), float(BIG))
    for d in range(D):
        tt(a("cmk", NG * d, NG * d + NG), ind(a("code", 128 * d, 128 * d + 128), a("blx")), a("mask"), Op.mult)
    tt(a("hi", 256, 384), a("lo", 0, 128), a("lo", 128, 256), Op.max)
    tt(a("hi", 384, 512), a("lo", 0, 128), a("lo", 128, 256), Op.min)
    ts(a("vB"), a("v16"), a("cf"), Op.add)
    tt(a("tri"), a("tri0"), a("gb"), Op.mult)
    for q in range(N):
        if q != r:
            act(a("od", 50 * q + 1, 50 * q + 49), slot("gidb", q, C))
    gather("s", a("od", 50 * r + 1, 50 * r + 49), a("gid"), a("se1", 0, 3))
    act(a("cs"), a("hi"), bias=float(TOP))
    fold16(a("k4", 0, 96), "gsf", "cmk", 0, 1536)

    gather("v", a("ptab1", G0, G0 + 192), a("od"), a("lu1", 0, 12))
    gather("s", a("ptab1", G0 + 192, TB), a("od"), a("lu1", 12, 24))
    tt(a("f1b"), ind(a("ptab1"), a("l1bu")), a("gidb"), Op.not_equal)
    send(2, "f1b", C, "ftab", G0)
    left2 = send(7, "xb", C, "xw", G0)
    iota(a("yw", V + 1024, 2 * V), [[0, 1024]], 0, 0)
    iota(a("vT"), [[0, 8], [1, 16]], 0, 16)
    dma("y", a("xo"), lambda: T.x[:, :], after=[left2])
    fold16(a("k5", 0, 24), "hb", "f1b", 0, NG)
    act(slot("ftab", r, C, G0), slot("f1b", r, C))
    for h in (0, 1):
        for d in range(3):
            act(a("csh", 192 * h + 64 * d, 192 * h + 64 * d + 64), a("cs", 128 * d + 64 * h, 128 * d + 64 * h + 64))
    act(a("hf"), a("hb"))
    act(a("hh"), a("hb"))
    act(a("q1b"), a("l1b"), bias=float(3 * 4096))
    act(a("q1"), a("l1s"), bias=float(TOP))
    act(slot("xw", r, C, G0), slot("xb", r, C))
    for name in ("xw", "ftab", "xt", "st"):
        act(a(name, 0, SH), a("jm", 0, SH), scale=0.0)
    act(a("ptab2", 0, SH), a("gid", 0, SH))
    act(a("nbu"), a("nbi"), bias=float(SH))
    act(a("idb"), a("zsl", 16, 144))
    act(a("idf"), a("zsl", 16, 144))
    act(a("zz"), a("jm"), scale=0.0)
    for k0, k1, t in PIECES[:-1]:
        act(a("st", 8 + 16 * k0, SH + 16 * k0), a("jm", 0, 8), scale=0.0)
    act(a("numt", 0, SH), a("jm", 0, SH), scale=0.0, bias=64.0)
    if r > 0:
        act(a("st", G0, me), a("gid", G0, me), scale=0.0)
    if r < 7:
        act(a("numg", low, NG), a("gid", me + C, TB), scale=0.0, bias=64.0)
    gather("s", a("wb", 0, low), a("w16"), a("blu", 0, low // 16))
    for h in (0, 1):
        c = SH + 1024 * h
        tt(a("ftab", c, c + 1024), ind(a("ptab1"), a("l1u", 64 * h, 64 * h + 64)), a("gid", c, c + 1024), Op.not_equal)
        fold16(a("k0", 64 * h, 64 * h + 64), "hb", "ftab", c, c + 1024)
    ts(a("codeb"), a("k4", 0, 96), float(TOP), Op.add)
    ts(a("nbba"), a("codeb"), 4095, Op.bitwise_and)
    tc(a("nbbu"), a("nbba"))
    ts(a("n3i"), a("cs", 0, 384), 4095, Op.bitwise_and)
    act(a("n3u"), a("n3i"))
    ts(a("m1bl"), a("k5", 0, 24), -1.0, Op.mult, 1.0, Op.add)
    ts(a("m1B"), a("k0", 0, 128), -1.0, Op.mult, 1.0, Op.add)
    tt(a("keepb"), a("q1b"), a("m1bl"), Op.mult)
    tt(a("keep"), a("q1"), a("m1B"), Op.mult)

    gather("s", a("fb", 0, 768), a("ftab"), a("nbbu", 0, 48))
    gather("v", a("fb", 768, 1536), a("ftab"), a("nbbu", 48, 96))
    fold16(a("k1", 0, 96), "hb", "fb", 0, 4 * NG)

    def flags(q, d, h, k0=0, k1=64):
        c, k = 1024 * (2 * d + h), 128 * d + 64 * h
        gather(q, a("fl", c + 16 * k0, c + 16 * k1), a("ftab"), a("n3u", k + k0, k + k1))

    def flagfold(d, h):
        c = 1024 * (2 * d + h)
        fold16(a("k%d" % (2 + h), 64 * d, 64 * d + 64), "hb", "fl", c, c + 1024)

    flags("s", 0, 0)
    flagfold(0, 0)
    for h in (0, 1):
        tt(a("key", 256 * h + 192, 256 * h + 256), a("cs", 384 + 64 * h, 448 + 64 * h), a("keep", 64 * h, 64 * h + 64), Op.max)
    flags("v", 2, 0, 0, 24)
    tt(a("kb"), a("codeb"), a("k1", 0, 96), Op.mult)
    tt(a("h2b"), a("kb", 0, 48), a("kb", 48, 96), Op.max)
    tt(a("h3b"), a("h2b", 0, 24), a("h2b", 24, 48), Op.max)
    tt(a("q2b"), a("h3b"), a("keepb"), Op.max)
    ts(a("l2bi"), a("q2b"), 4095, Op.bitwise_and)
    encode("out2", "d2", a("l2bi"), "rel2")
    left3 = send(3, "out2", 3, "lu2")
    iota(a("numt", SH, G0), [[0, V]], r, 0)
    flags("v", 2, 0, 24, 64)
    flagfold(2, 0)
    for c in range(16):
        dma("y", a("wa", p0=c, ps=16), lambda: T.w[:, 0:2 * V], after=[left3])
    flags("s", 1, 0)
    act(a("l2bu"), a("l2bi"))
    act(a("se2", 0, 3), slot("l2bi", r, 3))
    flagfold(1, 0)
    flags("s", 0, 1)
    flagfold(0, 1)

    def pointers(h):
        k, c = "k%d" % (2 + h), 64 * h
        tt(a("key", 4 * c, 4 * c + 192), a("csh", 3 * c, 3 * c + 192), a(k, 0, 192), Op.mult)
        tt(a("h2", 2 * c, 2 * c + 128), a("key", 4 * c, 4 * c + 128), a("key", 4 * c + 128, 4 * c + 256), Op.max)
        tt(a("q2", c, c + 64), a("h2", 2 * c, 2 * c + 64), a("h2", 2 * c + 64, 2 * c + 128), Op.max)
        ts(a("l2i", c, c + 64), a("q2", c, c + 64), 4095, Op.bitwise_and)
        tc(a("l2u", c, c + 64), a("l2i", c, c + 64))

    flags("v", 2, 1)
    flagfold(2, 1)
    pointers(0)
    flags("s", 1, 1, 0, 40)
    flags("v", 1, 1, 40, 64)
    flagfold(1, 1)
    gather("s", a("od", 50 * r + 1, 50 * r + 49), a("gid"), a("se2", 0, 3))
    gather("s", a("yc"), a("xw"), a("l2bu"))
    gather("v", a("ptab2", SH, SH + 384), a("gid"), a("l2u", 0, 24))
    gather("s", a("ptab2", SH + 384, SH + 1024), a("gid"), a("l2u", 24, 64))
    pointers(1)
    mm(a("k4", 0, NG), a("idb"), a("yc"))
    gather("v", a("ptab2", SH + 1024, SH + 1792), a("gid"), a("l2u", 64, 112))
    gather("s", a("ptab2", SH + 1792, G0), a("gid"), a("l2u", 112, 128))
    gather("s", a("ptab2", G0, TB), a("od"), a("lu2"))
    tt(a("m2b"), ind(a("ptab2"), a("l2bu")), a("gidb"), Op.is_equal)
    tt(a("xmb"), a("m2b"), a("k4", 0, NG), Op.mult)
    send(4, "xmb", C, "xm")
    for c in range(16):
        mm(a("k0", c, 128, 16), a("ptab2", SH + c, G0, 16), a("hf", 16, 144, 16))
    gather("s", a("pp2", 0, 1024), a("ptab2"), a("l2u", 0, 64))
    fold16(a("k6", 0, 64), "hh", "pp2", 0, 1024)
    gather("v", a("pp2", 1024, 1664), a("ptab2"), a("l2u", 64, 104))
    gather("s", a("pp2", 1664, 2048), a("ptab2"), a("l2u", 104, 128))
    fold16(a("k7", 0, 64), "hh", "pp2", 1024, 2048)

    def mates(h):
        c = 64 * h
        tt(a("m2B", c, c + 64), a("k%d" % (6 + h), 0, 64), a("vB", c, c + 64), Op.is_equal)
        tt(a("mu", c, c + 64), a("m2B", c, c + 64), a("l2i", c, c + 64), Op.mult)

    ts(a("pZ"), a("cf"), 1.0, Op.is_gt, 1000.0, Op.mult)
    ts(a("pS"), a("cf"), 2047.0, Op.mult, 1.0, Op.add)
    tt(a("gtc"), a("k0", 0, 128), a("vT"), Op.is_gt)
    tt(a("pY"), a("pZ"), a("p16"), Op.add)
    mates(0)
    ts(a("hh2"), a("jj", 0, 144), a("pY"), Op.is_equal, a("pS"), Op.mult)
    mm(a("k0", 0, 128), a("gtc"), a("idb"))
    act(slot("xm", r, C), slot("xmb", r, C))
    gather("s", a("xg"), a("xw"), a("mu", 0, XS // 16))
    mates(1)
    tt(a("rep"), a("k0", 0, 128), a("m2B"), Op.is_ge)
    mm(a("k0", 0, 128), a("gb"), a("rep"))
    mm(a("k0", 128, 256), a("tri"), a("rep"))
    for c in range(0, XS, 512):
        k, e = a("k%d" % (2 + c // 512), 0, min(512, XS - c)), min(XS, c + 512)
        mm(k, a("idb"), a("xo", c, e), True, False)
        mm(k, a("idb"), a("xg", c, e), False, True)
        act(a("xt", SH + c, SH + e), k)
    tt(a("xt", SH + XS, G0), ind(a("xw"), a("mu", XS // 16, 128)), a("xo", XS, V), Op.add)
    for k0, k1, t in PIECES:
        act(a("mur", k0, k1), a("mu", k0, k1), bias=-float(8 + 16 * k0), func=Fn.Relu)
    mm(a("k1", 0, NG), a("idb"), a("xw", G0, TB))
    for d in range(D):
        mm(a("k%d" % (4 + d), 0, low), a("sel", 128 * d, 128 * d + 128), a("wb", 0, low))
    op("v", lambda: g.vector.tensor_tensor_scan(ap(a("sc")), ap(a("k0", 0, 128)), ap(a("zz")), 0.0, Op.add, Op.add),
       [a("sc")], [a("k0", 0, 128), a("zz")])
    tt(a("nin"), a("sc"), a("k0", 128, 256), Op.add)
    mm(a("k0", 0, 128), a("nin"), a("zsl", 16, 144))
    act(a("ninT"), a("k0", 0, 128), bias=-1.0)
    for gr in range(8):
        dma("y", a("numt", SH, G0, p0=16 * gr, p1=16 * gr + 1), a("ninT", 16 * gr, 16 * gr + 16))
    act(a("na"), a("nin"), bias=float(V - 1))
    act(a("numf"), a("nin"), bias=float(V * r - 1))
    tt(a("xt", G0, TB), a("k1", 0, NG), a("xm"), Op.add)

    def near(i):
        k0, k1, t = PIECES[i]
        for d in range(NEAR[i]):
            tt(a("pr", V * d + 16 * k0, V * d + 16 * k1), ind(a("xt"), a("nbu", 128 * d + k0, 128 * d + k1)),
               a("wa", V * d + 16 * k0, V * d + 16 * k1), Op.mult)
        if JOIN[i]:
            x, y = a("pr", 16 * k0, 16 * k1), a("pr", V + 16 * k0, V + 16 * k1)
            op("g", lambda: g.dma_start(out=ap(x), in_=ap(y), accum_op=Op.add), [x], [x, y], inc=16)

    def wcast(i):
        k0, k1, t = PIECES[i]
        for d in range(NEAR[i], D):
            mm(a(BANKS[i][d], 0, 16 * (k1 - k0)), a("sel", 128 * d, 128 * d + 128), a("w16", 16 * k0, 16 * k1))

    def gather23(i):
        k0, k1, t = PIECES[i]
        for d in range(NEAR[i], D):
            gather("s", a("pr", V * d + 16 * k0, V * d + 16 * k1), a("xt"), a("nbu", 128 * d + k0, 128 * d + k1))

    def far(i):
        k0, k1, t = PIECES[i]
        p = [a("pr", V * d + 16 * k0, V * d + 16 * k1) for d in range(D)]
        k = a(BANKS[i][0], 0, 16 * (k1 - k0))
        out = a("st", SH + 16 * k0, SH + 16 * k1)
        for d in range(NEAR[i], D):
            tt(p[d], p[d], a(BANKS[i][d], 0, 16 * (k1 - k0)), Op.mult)
        if JOIN[i]:
            p = p[2:] + p[:1]
        for d in range(t):
            mm(k, a("idf"), p[d], d == 0, d == t - 1)

        def rest():
            for x in p[t:-1]:
                tt(k, x, k, Op.add)
            if t < len(p):
                tt(out, p[-1], k, Op.add)
            else:
                act(out, k)
        return rest

    wcast(0)
    near(0)
    gather23(0)
    end0 = far(0)
    for d in range(D):
        gather("s", a("cmk", NG * d, NG * d + low), a("xt"), a("nbbu", 24 * d, 24 * d + low // 16))
    b = [a("cmk", NG * d, NG * d + low) for d in range(D)]
    w = [a("k%d" % (4 + d), 0, low) for d in range(D)]
    tt(w[0], b[0], w[0], Op.mult)
    tt(a("nm"), a("na"), a("rep"), Op.mult)
    tt(b[1], b[1], w[1], Op.mult)
    tt(a("posu"), a("nm"), a("vB"), Op.max)
    tt(w[0], b[1], w[0], Op.add)
    tt(b[2], b[2], w[2], Op.mult)
    tt(b[3], b[3], w[3], Op.mult)
    tt(w[0], b[2], w[0], Op.add)
    tt(a("sb", 0, low), b[3], w[0], Op.add)
    send(5, "sb", C, "st", G0)
    wcast(1)
    wcast(2)
    gather23(1)
    near(1)
    end1 = far(1)
    wcast(3)
    gather23(2)
    gather("s", a("numb", high, NG), a("numt", SH, G0), a("blu", high // 16, 24))
    send(6, "numb", C, "numg")
    near(2)
    end0()
    gather23(3)
    act(slot("st", r, C, G0), slot("sb", r, C))
    end2 = far(2)
    near(3)
    last = []

    def mates_sums(i):
        k0 = PIECES[i][0]
        for c1, c0 in zip(CUTS[i], CUTS[i][1:]):
            gather("s", a("g2", 16 * c0, 16 * c1), a("st", 8 + 16 * k0, TB), a("mur", c0, c1))

    def scatter(i, part=None):
        cuts = CUTS[i] if part is None else CUTS[i][part:part + 2]
        for c1, c0 in zip(cuts, cuts[1:]):
            tt(ind(a("yw", 0, V + 16 * c1), a("posu", c0, c1)), a("st", SH + 16 * c0, SH + 16 * c1), a("g2", 16 * c0, 16 * c1), Op.add)
            last.append(dma("y", (lambda c0, c1: lambda: T.y[:, c0:c1])(16 * c0, 16 * c1), a("yw", V + 16 * c0, V + 16 * c1)))

    def mates_numbers(h):
        gather("s", a("nmate", 1024 * h, 1024 * h + 1024), a("numt"), a("mu", 64 * h, 64 * h + 64))
        fold16(a("k7", 64 * h, 64 * h + 64), "hh2", "nmate", 1024 * h, 1024 * h + 1024)

    act(slot("numg", r, C), slot("numb", r, C))
    mates_sums(0)
    end1()
    end3 = far(3)
    mates_sums(1)
    act(a("numt", G0, TB), a("numg"))
    mates_numbers(0)
    scatter(0)
    end2()
    mates_sums(2)
    mates_numbers(1)
    scatter(1)
    end3()
    mates_sums(3)
    scatter(2)
    tt(a("cmo"), a("k7", 0, 128), a("numf"), Op.min)
    last.append(dma("s", lambda: T.cm[:, :], a("cmo")))
    scatter(3)
    ops.append({"q": "y", "fn": None, "dep": set(last), "inc": 0, "sem": None, "waits": [], "K": 0})

    known = {q: 0 for q in "vstgy"}
    waiters = {}
    for i, o in enumerate(ops):
        if o["q"] == "r":
            continue
        k = known[o["q"]]
        for j in sorted(set(mmgroup.get(j, j) for j in o["dep"]), reverse=True):
            if not k >> j & 1:
                k |= ops[j]["K"] | 1 << j
                o["waits"].append(j)
                waiters.setdefault(j, []).append(i)
        known[o["q"]] = o["K"] = k
    groups = {}
    for j in sorted(waiters):
        if ops[j]["q"] != "r":
            groups.setdefault((ops[j]["q"], tuple(waiters[j])), []).append(j)
    pool, where, need = [], {}, {}
    for (q, ws), js in sorted(groups.items(), key=lambda t: t[1][0]):
        for s, p in enumerate(pool):
            if p[0] == q and all(all(ops[j]["K"] >> w & 1 or (ops[w]["q"] == q and w < j) for w in p[1]) for j in js):
                break
        else:
            s, p = len(pool), [q, (), 0]
            pool.append(p)
        p[1] = ws
        p[2] += sum(ops[j]["inc"] for j in js)
        for j in js:
            where[j], need[j] = "s%d" % s, p[2]
    assert len(pool) <= NPOOL, len(pool)
    for i, o in enumerate(ops):
        if o["q"] == "r":
            continue
        w = {}
        for j in o["waits"]:
            if ops[j]["q"] == "r":
                w[ops[j]["sem"]] = ops[j]["inc"]
            else:
                w[where[j]] = max(w.get(where[j], 0), need[j])
        for s in sorted(w):
            eng[o["q"]].wait_ge(T.sem[s], w[s])
        if o["fn"] is not None:
            x = o["fn"]()
            if i in where:
                x.then_inc(T.sem[where[i]], o["inc"])
    for k in range(8):
        if engines[k]:
            g.wait_ge(T.sem["t%d" % k], engines[k])
